import numpy as np
import ml_dtypes


def mxq(x, axis, fmt="e4m3"):
    dtype, down = {"e4m3": (ml_dtypes.float8_e4m3fn, 7), "e5m2": (ml_dtypes.float8_e5m2, 14)}[fmt]
    v = np.moveaxis(np.asarray(x, np.float32).astype(ml_dtypes.bfloat16).astype(np.float64), axis, -1)
    blocks = v.reshape(v.shape[:-1] + (-1, 32))
    amax = np.abs(blocks).max(-1, keepdims=True)
    byte = np.maximum(np.where(amax > 0, np.frexp(amax)[1] - 1 + 127, 0) - down, 1)
    scale = np.exp2(byte - 127.0)
    codes = (blocks / scale).astype(np.float32).astype(dtype).astype(np.float64)
    return np.moveaxis((codes * scale).reshape(v.shape), -1, axis)


WIDE = False


def mx_kscale(k):
    if not WIDE:
        return np.ones(k)
    levels = np.array([30, -30])
    if k % 512:
        return np.exp2(np.random.permutation(np.resize(levels, k // 32))).repeat(32)
    a = np.empty((k // 512, 16))
    for p in range(k // 512):
        a[p, :8] = np.random.permutation(np.resize(levels, 8))
        for g in range(8):
            far = levels[np.abs(levels - a[p, g]) >= 10]
            a[p, g + 8] = far[np.random.randint(len(far))]
    return np.exp2(a.ravel()).repeat(32)


def f64(x):
    return np.asarray(x).astype(np.float64)


def striped8(idx):
    return np.concatenate([v.reshape(-1, 16).T for v in idx]).astype(np.uint16)


def unstriped8(offs):
    return np.stack([offs[16 * g:16 * g + 16].T.reshape(-1) for g in range(8)]).astype(np.int64)


E2M1 = np.array([0.0, 0.5, 1.0, 1.5, 2.0, 3.0, 4.0, 6.0, -0.0, -0.5, -1.0, -1.5, -2.0, -3.0, -4.0, -6.0])


def pack_weight(w, fmt):
    k, n = w.shape
    w = f64(np.asarray(w, np.float32).astype(ml_dtypes.bfloat16)).reshape(k // 32, 32, n)
    amax = np.abs(w).max(1)
    if fmt == "e4m3":
        byte = np.frexp(amax)[1] - 1 + 127 - 7
    else:
        mant, ex = np.frexp(amax / 6.0)
        byte = np.where(mant > 0.5, ex, ex - 1) + 127
    byte = np.clip(np.where(amax > 0, byte, 1), 1, 254)
    scaled = (w * np.exp2(127.0 - byte)[:, None, :]).reshape(k, n).astype(np.float32)
    by_word = np.ascontiguousarray(scaled.reshape(k // 512, 128, 4, n).transpose(0, 1, 3, 2))
    if fmt == "e4m3":
        words = by_word.astype(ml_dtypes.float8_e4m3fn).view(np.uint8)
    else:
        c = by_word.astype(ml_dtypes.float4_e2m1fn).view(np.uint8) & 0xF
        words = (c[..., 0::2] | (c[..., 1::2] << 4)).reshape(k // 512, 128, 2 * n)
    return np.ascontiguousarray(words), np.ascontiguousarray(byte.astype(np.uint8).reshape(k // 512, 16, n))


def unpack_weight(words, scales, fmt):
    g, _, n = scales.shape
    words = np.ascontiguousarray(words).reshape(g, 128, n, -1)
    if fmt == "e4m3":
        vals = words.view(ml_dtypes.float8_e4m3fn).astype(np.float64)
    else:
        nib = np.empty((g, 128, n, 4), np.uint8)
        nib[..., 0::2] = words & 0xF
        nib[..., 1::2] = words >> 4
        vals = E2M1[nib]
    vals = vals * np.repeat(np.exp2(scales.astype(np.float64) - 127.0), 8, axis=1)[..., None]
    return vals.transpose(0, 1, 3, 2).reshape(g * 512, n)


K, N, T, J = 512, 1024, 2048, 1024


def setup_inputs():
    n = np.random.standard_normal
    s = mx_kscale(K)[:, None]
    m = np.exp(0.5 * n((1, J)))
    p_w4 = pack_weight(n((K, N)) / np.sqrt(K) / s, "e2m1")
    return {
        "dy": (m * n((K, J)) * s).astype(np.float32),
        "w4_words": p_w4[0],
        "w4_scales": p_w4[1],
        "wd": (0.4 * (n((K, N)) / np.sqrt(K) / s)).astype(np.float32),
        "wgo": np.repeat(np.random.uniform(0.5, 2.0, (8, J)), 16, axis=0).astype(np.float32),
        "offs": striped8(np.stack([np.random.permutation(T)[:J] for _ in range(8)])),
    }


def reference(dy, w4_words, w4_scales, wd, wgo, offs):
    idx = unstriped8(offs)
    dy_ = mxq(f64(dy), 0, "e5m2")
    w4_ = unpack_weight(w4_words, w4_scales, "e2m1")
    wd_ = mxq(f64(wd), 0, "e4m3")
    dx = w4_.T @ dy_ + wd_.T @ dy_
    out = np.zeros((N, T))
    rows = np.arange(N)
    out[rows[:, None], idx[rows % 128 // 16]] = f64(wgo)[rows % 128] * (dx)
    return out

@@ -1,0 +1,141 @@
+from contextlib import ExitStack
+
+import concourse.mybir as mybir
+
+K, N, T, J = 512, 1024, 2048, 1024
+FLOPS = 2 * 2 * K * N * J
+
+F32 = mybir.dt.float32
+BF16 = mybir.dt.bfloat16
+I32 = mybir.dt.int32
+U32 = mybir.dt.uint32
+U16 = mybir.dt.uint16
+U8 = mybir.dt.uint8
+E4M3 = mybir.dt.float8_e4m3fn_x4
+E5M2 = mybir.dt.float8_e5m2_x4
+E2M1 = mybir.dt.float4_e2m1fn_x4
+MULT = mybir.AluOpType.mult
+
+P = 128
+PACK = 4
+BANK = 512
+LIST_ROWS = 16
+BLOCKS = N // P
+PAGES = 3
+HEAD = 256
+VECTOR_COLUMNS = 160
+CLEAR = 512
+CHUNK = 128
+
+
+def tile_list_embg_dl_none_kernel(tc, dy, w4_words, w4_scales, wd, wgo, offs, out):
+    nc = tc.nc
+    with ExitStack() as ctx:
+        keep = ctx.enter_context(tc.tile_pool(name="keep", bufs=1))
+        psum = ctx.enter_context(tc.psum_pool(name="psum", bufs=8))
+
+        offsets = keep.tile([P, J // LIST_ROWS], U16, name="offsets")
+        w4_codes = keep.tile([P, 2 * N], U8, name="w4_codes", align_bytes=64)
+        w4_plane = keep.tile([P, N], U8, name="w4_plane", align_bytes=64)
+        wd_codes = keep.tile([P, N], U32, name="wd_codes", align_bytes=64)
+        wd_plane = keep.tile([P, N], U8, name="wd_plane", align_bytes=64)
+        dy_codes = keep.tile([P, HEAD + J], U32, name="dy_codes", align_bytes=64)
+        dy_plane = keep.tile([P, HEAD + J], U8, name="dy_plane", align_bytes=64)
+        weights = keep.tile([P, J], F32, name="weights")
+        pages = [keep.tile([P, T], F32, name="page%d" % i) for i in range(PAGES)]
+
+        def load(name, src, c0, c1):
+            raw = keep.tile([P, PACK, c1 - c0], F32, name="%s_raw%d" % (name, c0))
+            nc.sync.dma_start(out=raw[:], in_=src[:, c0:c1].rearrange("(p t) c -> p t c", t=PACK))
+            grouped = keep.tile([P, c1 - c0, PACK], BF16, name="%s_bf%d" % (name, c0), align_bytes=64)
+            return raw, grouped, c0, c1
+
+        def weave(piece, copy, a, b):
+            raw, grouped = piece[0], piece[1]
+            copy(out=grouped[:, a:b, :], in_=raw[:, :, a:b].rearrange("p t c -> p c t"))
+
+        def weave_on_scalar(piece):
+            for a in range(0, piece[3] - piece[2], CHUNK):
+                weave(piece, nc.scalar.copy, a, a + CHUNK)
+
+        def weave_on_both(piece):
+            weave(piece, nc.vector.tensor_copy, 0, VECTOR_COLUMNS)
+            weave(piece, nc.scalar.copy, VECTOR_COLUMNS, piece[3] - piece[2])
+
+        def quantise(piece, codes, plane, fmt, shift):
+            grouped, c0, c1 = piece[1], piece[2] + shift, piece[3] + shift
+            nc.vector.quantize_mx(out=codes[:, c0:c1].bitcast(fmt), scales=plane[:, c0:c1],
+                                  in_=grouped[:].rearrange("p c t -> p (c t)"))
+
+        def multiply(b, first):
+            rows = slice(b * P, (b + 1) * P)
+            cols = slice(HEAD + first, HEAD + first + BANK)
+            acc = psum.tile([P, BANK], F32, name="acc")
+            moving = dy_codes[:, cols].bitcast(E5M2)
+            nc.tensor.matmul_mx(out=acc[:], lhsT=wd_codes[:, rows].bitcast(E4M3), lhsT_scale=wd_plane[:, rows],
+                                rhs=moving, rhs_scale=dy_plane[:, cols], start=True, stop=False)
+            nc.tensor.matmul_mx(out=acc[:], lhsT=w4_codes[:, 2 * b * P : 2 * (b + 1) * P].bitcast(E2M1),
+                                lhsT_scale=w4_plane[:, rows], rhs=moving, rhs_scale=dy_plane[:, cols],
+                                start=False, stop=True)
+            return acc
+
+        def clear(page):
+            for a in range(0, T, CLEAR):
+                nc.vector.memset(page[:, a : a + CLEAR].bitcast(U32), 0)
+
+        def place(b, c0, c1, tag):
+            sums = keep.tile([P, c1 - c0], F32, name="sums", tag=tag)
+            for first in range(c1 - BANK * -(-(c1 - c0) // BANK), c1, BANK):
+                acc = multiply(b, first)
+                a = max(first, c0)
+                nc.scalar.copy(out=sums[:, a - c0 : first + BANK - c0], in_=acc[:, a - first :])
+            window = pages[b % PAGES][:].indirect(offsets[:, c0 // LIST_ROWS : c1 // LIST_ROWS])
+            nc.vector.tensor_tensor(window, sums[:], weights[:, c0:c1], MULT)
+            if c1 == J:
+                nc.sync.dma_start(out=out[b * P : (b + 1) * P, :], in_=pages[b % PAGES][:])
+
+        nc.vector.memset(w4_plane[:].bitcast(U32), 0)
+        nc.vector.memset(dy_codes[:, :HEAD], 0)
+        nc.vector.memset(dy_plane[:, :HEAD].bitcast(U32), 0)
+        words = w4_words[0].bitcast(I32)
+        codes_i32 = w4_codes[:].bitcast(I32)
+
+        wd01 = load("wd", wd, 0, 2 * P)
+        nc.sync.dma_start(out=codes_i32[:, :P], in_=words[:, :P])
+        dy_a = load("dy", dy, 0, HEAD)
+        dy_b = load("dy", dy, HEAD, BANK)
+        for q in range(4):
+            nc.scalar.dma_start(out=w4_plane[32 * q : 32 * q + 4, :].bitcast(I32),
+                                in_=w4_scales[0, 4 * q : 4 * q + 4, :].bitcast(I32))
+        nc.sync.dma_start(offsets[:], offs)
+        nc.sync.dma_start(out=weights[:, :BANK], in_=wgo[:, :BANK])
+        wd23 = load("wd", wd, 2 * P, 4 * P)
+        nc.sync.dma_start(out=codes_i32[:, P:], in_=words[:, P:])
+        dy_c = load("dy", dy, BANK, J)
+        nc.sync.dma_start(out=weights[:, BANK:], in_=wgo[:, BANK:])
+        wd47 = load("wd", wd, 4 * P, N)
+
+        clear(pages[0])
+        weave_on_scalar(wd01)
+        quantise(wd01, wd_codes, wd_plane, E4M3, 0)
+        weave_on_both(dy_a)
+        quantise(dy_a, dy_codes, dy_plane, E5M2, HEAD)
+        place(0, 0, HEAD, "s0a")
+        weave_on_both(dy_b)
+        quantise(dy_b, dy_codes, dy_plane, E5M2, HEAD)
+        place(0, HEAD, BANK, "s0b")
+        clear(pages[1])
+        weave_on_scalar(wd23)
+        quantise(wd23, wd_codes, wd_plane, E4M3, 0)
+        place(1, 0, BANK, "wd_raw256")
+        clear(pages[2])
+        weave_on_scalar(dy_c)
+        quantise(dy_c, dy_codes, dy_plane, E5M2, HEAD)
+        place(2, 0, BANK, "dy_raw512")
+        place(0, BANK, J, "s0c")
+        weave_on_scalar(wd47)
+        quantise(wd47, wd_codes, wd_plane, E4M3, 0)
+        place(1, BANK, J, "wd_raw512")
+        place(2, BANK, J, "s2c")
+        for b in range(PAGES, BLOCKS):
+            place(b, 0, J, "s%d" % b)

@@ -21,10 +21,11 @@ PACK = 4
 BANK = 512
 LIST_ROWS = 16
 BLOCKS = N // P
-PAGES = 3
+PAGES = 2
 HEAD = 256
-VECTOR_COLUMNS = 160
-CLEAR = 512
+VECTOR_COLUMNS = 176
+SPLIT = 160
+ODD = T // 2 - 1
 CHUNK = 128
 
 
@@ -37,7 +38,7 @@ def tile_list_embg_dl_none_kernel(tc, dy, w4_words, w4_scales, wd, wgo, offs, ou
         offsets = keep.tile([P, J // LIST_ROWS], U16, name="offsets")
         w4_codes = keep.tile([P, 2 * N], U8, name="w4_codes", align_bytes=64)
         w4_plane = keep.tile([P, N], U8, name="w4_plane", align_bytes=64)
-        wd_codes = keep.tile([P, N], U32, name="wd_codes", align_bytes=64)
+        wd_codes = {}
         wd_plane = keep.tile([P, N], U8, name="wd_plane", align_bytes=64)
         dy_codes = keep.tile([P, HEAD + J], U32, name="dy_codes", align_bytes=64)
         dy_plane = keep.tile([P, HEAD + J], U8, name="dy_plane", align_bytes=64)
@@ -45,7 +46,7 @@ def tile_list_embg_dl_none_kernel(tc, dy, w4_words, w4_scales, wd, wgo, offs, ou
         pages = [keep.tile([P, T], F32, name="page%d" % i) for i in range(PAGES)]
 
         def load(name, src, c0, c1):
-            raw = keep.tile([P, PACK, c1 - c0], F32, name="%s_raw%d" % (name, c0))
+            raw = keep.tile([P, PACK, c1 - c0], F32, name="%s_raw%d" % (name, c0), align_bytes=64)
             nc.sync.dma_start(out=raw[:], in_=src[:, c0:c1].rearrange("(p t) c -> p t c", t=PACK))
             grouped = keep.tile([P, c1 - c0, PACK], BF16, name="%s_bf%d" % (name, c0), align_bytes=64)
             return raw, grouped, c0, c1
@@ -59,83 +60,96 @@ def tile_list_embg_dl_none_kernel(tc, dy, w4_words, w4_scales, wd, wgo, offs, ou
                 weave(piece, nc.scalar.copy, a, a + CHUNK)
 
         def weave_on_both(piece):
-            weave(piece, nc.vector.tensor_copy, 0, VECTOR_COLUMNS)
-            weave(piece, nc.scalar.copy, VECTOR_COLUMNS, piece[3] - piece[2])
+            width = piece[3] - piece[2]
+            cut = width * VECTOR_COLUMNS // HEAD
+            weave(piece, nc.vector.tensor_copy, 0, cut)
+            weave(piece, nc.scalar.copy, cut, width)
 
-        def quantise(piece, codes, plane, fmt, shift):
-            grouped, c0, c1 = piece[1], piece[2] + shift, piece[3] + shift
-            nc.vector.quantize_mx(out=codes[:, c0:c1].bitcast(fmt), scales=plane[:, c0:c1],
-                                  in_=grouped[:].rearrange("p c t -> p (c t)"))
+        def quantise(piece, codes, plane, fmt):
+            nc.vector.quantize_mx(out=codes.bitcast(fmt), scales=plane, in_=piece[1][:].rearrange("p c t -> p (c t)"))
+
+        def quantise_dy(piece):
+            cols = slice(HEAD + piece[2], HEAD + piece[3])
+            quantise(piece, dy_codes[:, cols], dy_plane[:, cols], E5M2)
+
+        def quantise_wd(piece, tag):
+            c0, c1 = piece[2], piece[3]
+            codes = keep.tile([P, c1 - c0], U32, name="wd_codes", tag=tag, align_bytes=64)
+            quantise(piece, codes[:], wd_plane[:, c0:c1], E4M3)
+            wd_codes.update({b: codes[:, b * P - c0 : (b + 1) * P - c0] for b in range(c0 // P, c1 // P)})
 
         def multiply(b, first):
             rows = slice(b * P, (b + 1) * P)
             cols = slice(HEAD + first, HEAD + first + BANK)
             acc = psum.tile([P, BANK], F32, name="acc")
             moving = dy_codes[:, cols].bitcast(E5M2)
-            nc.tensor.matmul_mx(out=acc[:], lhsT=wd_codes[:, rows].bitcast(E4M3), lhsT_scale=wd_plane[:, rows],
-                                rhs=moving, rhs_scale=dy_plane[:, cols], start=True, stop=False)
             nc.tensor.matmul_mx(out=acc[:], lhsT=w4_codes[:, 2 * b * P : 2 * (b + 1) * P].bitcast(E2M1),
                                 lhsT_scale=w4_plane[:, rows], rhs=moving, rhs_scale=dy_plane[:, cols],
-                                start=False, stop=True)
-            return acc
+                                start=True, stop=False)
+            nc.tensor.matmul_mx(out=acc[:], lhsT=wd_codes[b].bitcast(E4M3), lhsT_scale=wd_plane[:, rows],
+                                rhs=moving, rhs_scale=dy_plane[:, cols], start=False, stop=True)
+            return [(first, acc)]
 
-        def clear(page):
-            for a in range(0, T, CLEAR):
-                nc.vector.memset(page[:, a : a + CLEAR].bitcast(U32), 0)
-
-        def place(b, c0, c1, tag):
-            sums = keep.tile([P, c1 - c0], F32, name="sums", tag=tag)
-            for first in range(c1 - BANK * -(-(c1 - c0) // BANK), c1, BANK):
-                acc = multiply(b, first)
-                a = max(first, c0)
-                nc.scalar.copy(out=sums[:, a - c0 : first + BANK - c0], in_=acc[:, a - first :])
+        def place(b, c0, c1, tag, banks):
+            sums = keep.tile([P, c1 - c0], F32, name="sums", tag=tag, align_bytes=64)
+            for first, acc in banks:
+                a, z = max(first, c0), min(first + BANK, c1)
+                nc.scalar.copy(out=sums[:, a - c0 : z - c0], in_=acc[:, a - first : z - first])
             window = pages[b % PAGES][:].indirect(offsets[:, c0 // LIST_ROWS : c1 // LIST_ROWS])
             nc.vector.tensor_tensor(window, sums[:], weights[:, c0:c1], MULT)
             if c1 == J:
                 nc.sync.dma_start(out=out[b * P : (b + 1) * P, :], in_=pages[b % PAGES][:])
+            return sums
 
-        nc.vector.memset(w4_plane[:].bitcast(U32), 0)
-        nc.vector.memset(dy_codes[:, :HEAD], 0)
-        nc.vector.memset(dy_plane[:, :HEAD].bitcast(U32), 0)
+        nc.gpsimd.memset(w4_plane[:].bitcast(U32), 0)
+        nc.gpsimd.memset(dy_codes[:, :HEAD], 0)
+        nc.gpsimd.memset(dy_plane[:, :HEAD].bitcast(U32), 0)
+        nc.gpsimd.memset(pages[1][:], 0.0)
+        nc.vector.memset(pages[0][:, :ODD], 0.0)
+        nc.vector.memset(pages[0][:, ODD:], 0.0)
         words = w4_words[0].bitcast(I32)
         codes_i32 = w4_codes[:].bitcast(I32)
 
-        wd01 = load("wd", wd, 0, 2 * P)
-        nc.sync.dma_start(out=codes_i32[:, :P], in_=words[:, :P])
         dy_a = load("dy", dy, 0, HEAD)
-        dy_b = load("dy", dy, HEAD, BANK)
         for q in range(4):
-            nc.scalar.dma_start(out=w4_plane[32 * q : 32 * q + 4, :].bitcast(I32),
-                                in_=w4_scales[0, 4 * q : 4 * q + 4, :].bitcast(I32))
+            nc.sync.dma_start(out=w4_plane[32 * q : 32 * q + 4, :].bitcast(I32),
+                              in_=w4_scales[0, 4 * q : 4 * q + 4, :].bitcast(I32))
+        nc.sync.dma_start(out=codes_i32[:, :P], in_=words[:, :P])
+        wd0 = load("wd", wd, 0, P)
+        dy_b = load("dy", dy, HEAD, BANK)
         nc.sync.dma_start(offsets[:], offs)
-        nc.sync.dma_start(out=weights[:, :BANK], in_=wgo[:, :BANK])
-        wd23 = load("wd", wd, 2 * P, 4 * P)
-        nc.sync.dma_start(out=codes_i32[:, P:], in_=words[:, P:])
-        dy_c = load("dy", dy, BANK, J)
+        nc.sync.dma_start(out=weights[:, :HEAD], in_=wgo[:, :HEAD])
+        wd1 = load("wd", wd, P, 2 * P)
+        nc.sync.dma_start(out=weights[:, HEAD:BANK], in_=wgo[:, HEAD:BANK])
+        dy_c = load("dy", dy, BANK, BANK + HEAD)
+        dy_d = load("dy", dy, BANK + HEAD, J)
         nc.sync.dma_start(out=weights[:, BANK:], in_=wgo[:, BANK:])
+        nc.sync.dma_start(out=codes_i32[:, P:], in_=words[:, P:])
+        wd23 = load("wd", wd, 2 * P, 4 * P)
         wd47 = load("wd", wd, 4 * P, N)
 
-        clear(pages[0])
-        weave_on_scalar(wd01)
-        quantise(wd01, wd_codes, wd_plane, E4M3, 0)
         weave_on_both(dy_a)
-        quantise(dy_a, dy_codes, dy_plane, E5M2, HEAD)
-        place(0, 0, HEAD, "s0a")
+        quantise_dy(dy_a)
+        weave_on_both(wd0)
+        quantise_wd(wd0, "wd_codes0")
+        first_group = multiply(0, -HEAD)
         weave_on_both(dy_b)
-        quantise(dy_b, dy_codes, dy_plane, E5M2, HEAD)
-        place(0, HEAD, BANK, "s0b")
-        clear(pages[1])
+        quantise_dy(dy_b)
+        s0a = place(0, 0, HEAD, "dy_raw256", first_group)
+        weave_on_scalar(wd1)
+        quantise_wd(wd1, "wd_codes1")
+        s0b = place(0, HEAD, BANK, "wd_raw128", multiply(0, 0))
+        left = multiply(1, 0)
+        place(1, 0, SPLIT, "s1a", left)
+        for piece in (dy_c, dy_d):
+            weave_on_scalar(piece)
+            quantise_dy(piece)
+        place(1, SPLIT, BANK, "dy_raw768", left)
+        place(0, BANK, J, "s0c", multiply(0, BANK))
         weave_on_scalar(wd23)
-        quantise(wd23, wd_codes, wd_plane, E4M3, 0)
-        place(1, 0, BANK, "wd_raw256")
-        clear(pages[2])
-        weave_on_scalar(dy_c)
-        quantise(dy_c, dy_codes, dy_plane, E5M2, HEAD)
-        place(2, 0, BANK, "dy_raw512")
-        place(0, BANK, J, "s0c")
+        quantise_wd(wd23, "s0c")
+        place(1, BANK, J, "s1c", multiply(1, BANK))
         weave_on_scalar(wd47)
-        quantise(wd47, wd_codes, wd_plane, E4M3, 0)
-        place(1, BANK, J, "wd_raw512")
-        place(2, BANK, J, "s2c")
+        quantise_wd(wd47, "s1c")
         for b in range(PAGES, BLOCKS):
-            place(b, 0, J, "s%d" % b)
+            place(b, 0, J, "s%d" % b, multiply(b, 0) + multiply(b, BANK))

@@ -21,11 +21,10 @@ PACK = 4
 BANK = 512
 LIST_ROWS = 16
 BLOCKS = N // P
-PAGES = 2
+PAGES = 3
 HEAD = 256
 VECTOR_COLUMNS = 176
-SPLIT = 160
-ODD = T // 2 - 1
+CLEAR = 512
 CHUNK = 128
 
 
@@ -43,7 +42,7 @@ def tile_list_embg_dl_none_kernel(tc, dy, w4_words, w4_scales, wd, wgo, offs, ou
         dy_codes = keep.tile([P, HEAD + J], U32, name="dy_codes", align_bytes=64)
         dy_plane = keep.tile([P, HEAD + J], U8, name="dy_plane", align_bytes=64)
         weights = keep.tile([P, J], F32, name="weights")
-        pages = [keep.tile([P, T], F32, name="page%d" % i) for i in range(PAGES)]
+        pages = [keep.tile([P, T], F32, name="page%d" % i) for i in range(PAGES - 1)]
 
         def load(name, src, c0, c1):
             raw = keep.tile([P, PACK, c1 - c0], F32, name="%s_raw%d" % (name, c0), align_bytes=64)
@@ -101,12 +100,10 @@ def tile_list_embg_dl_none_kernel(tc, dy, w4_words, w4_scales, wd, wgo, offs, ou
                 nc.sync.dma_start(out=out[b * P : (b + 1) * P, :], in_=pages[b % PAGES][:])
             return sums
 
-        nc.gpsimd.memset(w4_plane[:].bitcast(U32), 0)
-        nc.gpsimd.memset(dy_codes[:, :HEAD], 0)
-        nc.gpsimd.memset(dy_plane[:, :HEAD].bitcast(U32), 0)
-        nc.gpsimd.memset(pages[1][:], 0.0)
-        nc.vector.memset(pages[0][:, :ODD], 0.0)
-        nc.vector.memset(pages[0][:, ODD:], 0.0)
+        nc.vector.memset(w4_plane[:].bitcast(U32), 0)
+        nc.vector.memset(dy_codes[:, :HEAD], 0)
+        nc.vector.memset(dy_plane[:, :HEAD].bitcast(U32), 0)
+        nc.vector.memset(pages[0][:], 0.0)
         words = w4_words[0].bitcast(I32)
         codes_i32 = w4_codes[:].bitcast(I32)
 
@@ -118,14 +115,12 @@ def tile_list_embg_dl_none_kernel(tc, dy, w4_words, w4_scales, wd, wgo, offs, ou
         wd0 = load("wd", wd, 0, P)
         dy_b = load("dy", dy, HEAD, BANK)
         nc.sync.dma_start(offsets[:], offs)
-        nc.sync.dma_start(out=weights[:, :HEAD], in_=wgo[:, :HEAD])
-        wd1 = load("wd", wd, P, 2 * P)
-        nc.sync.dma_start(out=weights[:, HEAD:BANK], in_=wgo[:, HEAD:BANK])
-        dy_c = load("dy", dy, BANK, BANK + HEAD)
-        dy_d = load("dy", dy, BANK + HEAD, J)
-        nc.sync.dma_start(out=weights[:, BANK:], in_=wgo[:, BANK:])
+        nc.sync.dma_start(out=weights[:, :BANK], in_=wgo[:, :BANK])
+        wd12 = load("wd", wd, P, 3 * P)
         nc.sync.dma_start(out=codes_i32[:, P:], in_=words[:, P:])
-        wd23 = load("wd", wd, 2 * P, 4 * P)
+        dy_c = load("dy", dy, BANK, J)
+        nc.sync.dma_start(out=weights[:, BANK:], in_=wgo[:, BANK:])
+        wd3 = load("wd", wd, 3 * P, 4 * P)
         wd47 = load("wd", wd, 4 * P, N)
 
         weave_on_both(dy_a)
@@ -136,20 +131,23 @@ def tile_list_embg_dl_none_kernel(tc, dy, w4_words, w4_scales, wd, wgo, offs, ou
         weave_on_both(dy_b)
         quantise_dy(dy_b)
         s0a = place(0, 0, HEAD, "dy_raw256", first_group)
-        weave_on_scalar(wd1)
-        quantise_wd(wd1, "wd_codes1")
+        for a in range(0, T, CLEAR):
+            nc.vector.memset(pages[1][:, a : a + CLEAR], 0.0)
+        weave_on_scalar(wd12)
+        quantise_wd(wd12, "wd_codes1")
+        pages.append(keep.tile([P, T], F32, name="page2", tag="wd_bf128", align_bytes=64))
+        for a in range(0, T, CLEAR):
+            nc.gpsimd.memset(pages[2][:, a : a + CLEAR], 0.0)
         s0b = place(0, HEAD, BANK, "wd_raw128", multiply(0, 0))
-        left = multiply(1, 0)
-        place(1, 0, SPLIT, "s1a", left)
-        for piece in (dy_c, dy_d):
-            weave_on_scalar(piece)
-            quantise_dy(piece)
-        place(1, SPLIT, BANK, "dy_raw768", left)
+        place(1, 0, BANK, "s1a", multiply(1, 0))
+        weave_on_scalar(dy_c)
+        quantise_dy(dy_c)
+        place(2, 0, BANK, "dy_raw512", multiply(2, 0))
         place(0, BANK, J, "s0c", multiply(0, BANK))
-        weave_on_scalar(wd23)
-        quantise_wd(wd23, "s0c")
-        place(1, BANK, J, "s1c", multiply(1, BANK))
-        weave_on_scalar(wd47)
-        quantise_wd(wd47, "s1c")
+        for piece in (wd3, wd47):
+            weave_on_scalar(piece)
+            quantise_wd(piece, "wd_codes%d" % piece[2])
+        place(1, BANK, J, "wd_raw512", multiply(1, BANK))
+        place(2, BANK, J, "s2c", multiply(2, BANK))
         for b in range(PAGES, BLOCKS):
             place(b, 0, J, "s%d" % b, multiply(b, 0) + multiply(b, BANK))

@@ -19,20 +19,23 @@ MULT = mybir.AluOpType.mult
 P = 128
 PACK = 4
 BANK = 512
+PSUM_BANKS = 8
+QUADRANTS = 4
 LIST_ROWS = 16
 BLOCKS = N // P
 PAGES = 3
 HEAD = 256
 VECTOR_COLUMNS = 176
-CLEAR = 512
+CLEAR = 256
 CHUNK = 128
+W4_FIRST = 2 * P // 2
 
 
 def tile_list_embg_dl_none_kernel(tc, dy, w4_words, w4_scales, wd, wgo, offs, out):
     nc = tc.nc
     with ExitStack() as ctx:
         keep = ctx.enter_context(tc.tile_pool(name="keep", bufs=1))
-        psum = ctx.enter_context(tc.psum_pool(name="psum", bufs=8))
+        psum = ctx.enter_context(tc.psum_pool(name="psum", bufs=PSUM_BANKS))
 
         offsets = keep.tile([P, J // LIST_ROWS], U16, name="offsets")
         w4_codes = keep.tile([P, 2 * N], U8, name="w4_codes", align_bytes=64)
@@ -42,7 +45,7 @@ def tile_list_embg_dl_none_kernel(tc, dy, w4_words, w4_scales, wd, wgo, offs, ou
         dy_codes = keep.tile([P, HEAD + J], U32, name="dy_codes", align_bytes=64)
         dy_plane = keep.tile([P, HEAD + J], U8, name="dy_plane", align_bytes=64)
         weights = keep.tile([P, J], F32, name="weights")
-        pages = [keep.tile([P, T], F32, name="page%d" % i) for i in range(PAGES - 1)]
+        pages = [keep.tile([P, T], F32, name="page0")]
 
         def load(name, src, c0, c1):
             raw = keep.tile([P, PACK, c1 - c0], F32, name="%s_raw%d" % (name, c0), align_bytes=64)
@@ -50,13 +53,13 @@ def tile_list_embg_dl_none_kernel(tc, dy, w4_words, w4_scales, wd, wgo, offs, ou
             grouped = keep.tile([P, c1 - c0, PACK], BF16, name="%s_bf%d" % (name, c0), align_bytes=64)
             return raw, grouped, c0, c1
 
-        def weave(piece, copy, a, b):
-            raw, grouped = piece[0], piece[1]
-            copy(out=grouped[:, a:b, :], in_=raw[:, :, a:b].rearrange("p t c -> p c t"))
+        def weave(piece, copy, lo, hi):
+            raw, grouped = piece[:2]
+            copy(out=grouped[:, lo:hi, :], in_=raw[:, :, lo:hi].rearrange("p t c -> p c t"))
 
         def weave_on_scalar(piece):
-            for a in range(0, piece[3] - piece[2], CHUNK):
-                weave(piece, nc.scalar.copy, a, a + CHUNK)
+            for lo in range(0, piece[3] - piece[2], CHUNK):
+                weave(piece, nc.scalar.copy, lo, lo + CHUNK)
 
         def weave_on_both(piece):
             width = piece[3] - piece[2]
@@ -65,15 +68,16 @@ def tile_list_embg_dl_none_kernel(tc, dy, w4_words, w4_scales, wd, wgo, offs, ou
             weave(piece, nc.scalar.copy, cut, width)
 
         def quantise(piece, codes, plane, fmt):
-            nc.vector.quantize_mx(out=codes.bitcast(fmt), scales=plane, in_=piece[1][:].rearrange("p c t -> p (c t)"))
+            grouped = piece[1]
+            nc.vector.quantize_mx(out=codes.bitcast(fmt), scales=plane, in_=grouped[:].rearrange("p c t -> p (c t)"))
 
         def quantise_dy(piece):
             cols = slice(HEAD + piece[2], HEAD + piece[3])
             quantise(piece, dy_codes[:, cols], dy_plane[:, cols], E5M2)
 
-        def quantise_wd(piece, tag):
-            c0, c1 = piece[2], piece[3]
-            codes = keep.tile([P, c1 - c0], U32, name="wd_codes", tag=tag, align_bytes=64)
+        def quantise_wd(piece):
+            c0, c1 = piece[2:]
+            codes = keep.tile([P, c1 - c0], U32, name="wd_codes%d" % c0, align_bytes=64)
             quantise(piece, codes[:], wd_plane[:, c0:c1], E4M3)
             wd_codes.update({b: codes[:, b * P - c0 : (b + 1) * P - c0] for b in range(c0 // P, c1 // P)})
 
@@ -92,32 +96,37 @@ def tile_list_embg_dl_none_kernel(tc, dy, w4_words, w4_scales, wd, wgo, offs, ou
         def place(b, c0, c1, tag, banks):
             sums = keep.tile([P, c1 - c0], F32, name="sums", tag=tag, align_bytes=64)
             for first, acc in banks:
-                a, z = max(first, c0), min(first + BANK, c1)
-                nc.scalar.copy(out=sums[:, a - c0 : z - c0], in_=acc[:, a - first : z - first])
+                lo, hi = max(first, c0), min(first + BANK, c1)
+                nc.scalar.copy(out=sums[:, lo - c0 : hi - c0], in_=acc[:, lo - first : hi - first])
             window = pages[b % PAGES][:].indirect(offsets[:, c0 // LIST_ROWS : c1 // LIST_ROWS])
             nc.vector.tensor_tensor(window, sums[:], weights[:, c0:c1], MULT)
             if c1 == J:
                 nc.sync.dma_start(out=out[b * P : (b + 1) * P, :], in_=pages[b % PAGES][:])
-            return sums
+
+        def clear_on_gpsimd(tag):
+            page = keep.tile([P, T], F32, name="page", tag=tag, align_bytes=64)
+            pages.append(page)
+            for lo in range(0, T, CLEAR):
+                nc.gpsimd.memset(page[:, lo : lo + CLEAR], 0.0)
 
         nc.vector.memset(w4_plane[:].bitcast(U32), 0)
         nc.vector.memset(dy_codes[:, :HEAD], 0)
         nc.vector.memset(dy_plane[:, :HEAD].bitcast(U32), 0)
         nc.vector.memset(pages[0][:], 0.0)
-        words = w4_words[0].bitcast(I32)
-        codes_i32 = w4_codes[:].bitcast(I32)
 
+        words_hbm = w4_words[0].bitcast(I32)
+        words_sbuf = w4_codes[:].bitcast(I32)
         dy_a = load("dy", dy, 0, HEAD)
-        for q in range(4):
+        nc.sync.dma_start(out=words_sbuf[:, :W4_FIRST], in_=words_hbm[:, :W4_FIRST])
+        wd0 = load("wd", wd, 0, P)
+        for q in range(QUADRANTS):
             nc.sync.dma_start(out=w4_plane[32 * q : 32 * q + 4, :].bitcast(I32),
                               in_=w4_scales[0, 4 * q : 4 * q + 4, :].bitcast(I32))
-        nc.sync.dma_start(out=codes_i32[:, :P], in_=words[:, :P])
-        wd0 = load("wd", wd, 0, P)
         dy_b = load("dy", dy, HEAD, BANK)
         nc.sync.dma_start(offsets[:], offs)
         nc.sync.dma_start(out=weights[:, :BANK], in_=wgo[:, :BANK])
         wd12 = load("wd", wd, P, 3 * P)
-        nc.sync.dma_start(out=codes_i32[:, P:], in_=words[:, P:])
+        nc.sync.dma_start(out=words_sbuf[:, W4_FIRST:], in_=words_hbm[:, W4_FIRST:])
         dy_c = load("dy", dy, BANK, J)
         nc.sync.dma_start(out=weights[:, BANK:], in_=wgo[:, BANK:])
         wd3 = load("wd", wd, 3 * P, 4 * P)
@@ -126,28 +135,28 @@ def tile_list_embg_dl_none_kernel(tc, dy, w4_words, w4_scales, wd, wgo, offs, ou
         weave_on_both(dy_a)
         quantise_dy(dy_a)
         weave_on_both(wd0)
-        quantise_wd(wd0, "wd_codes0")
-        first_group = multiply(0, -HEAD)
+        quantise_wd(wd0)
+        padded = multiply(0, -HEAD)
         weave_on_both(dy_b)
         quantise_dy(dy_b)
-        s0a = place(0, 0, HEAD, "dy_raw256", first_group)
-        for a in range(0, T, CLEAR):
-            nc.vector.memset(pages[1][:, a : a + CLEAR], 0.0)
+        place(0, 0, HEAD, "dy_raw256", padded)
+        clear_on_gpsimd("dy_bf256")
+
         weave_on_scalar(wd12)
-        quantise_wd(wd12, "wd_codes1")
-        pages.append(keep.tile([P, T], F32, name="page2", tag="wd_bf128", align_bytes=64))
-        for a in range(0, T, CLEAR):
-            nc.gpsimd.memset(pages[2][:, a : a + CLEAR], 0.0)
-        s0b = place(0, HEAD, BANK, "wd_raw128", multiply(0, 0))
-        place(1, 0, BANK, "s1a", multiply(1, 0))
+        quantise_wd(wd12)
+        clear_on_gpsimd("wd_bf128")
+        place(0, HEAD, BANK, "wd_raw128", multiply(0, 0))
+        place(1, 0, BANK, "sums1a", multiply(1, 0))
         weave_on_scalar(dy_c)
         quantise_dy(dy_c)
         place(2, 0, BANK, "dy_raw512", multiply(2, 0))
-        place(0, BANK, J, "s0c", multiply(0, BANK))
+
+        place(0, BANK, J, "sums0c", multiply(0, BANK))
         for piece in (wd3, wd47):
             weave_on_scalar(piece)
-            quantise_wd(piece, "wd_codes%d" % piece[2])
+            quantise_wd(piece)
         place(1, BANK, J, "wd_raw512", multiply(1, BANK))
-        place(2, BANK, J, "s2c", multiply(2, BANK))
+        place(2, BANK, J, "sums2b", multiply(2, BANK))
+
         for b in range(PAGES, BLOCKS):
-            place(b, 0, J, "s%d" % b, multiply(b, 0) + multiply(b, BANK))
+            place(b, 0, J, "sums%d" % b, multiply(b, 0) + multiply(b, BANK))

@@ -23,7 +23,7 @@ PSUM_BANKS = 8
 QUADRANTS = 4
 LIST_ROWS = 16
 BLOCKS = N // P
-PAGES = 3
+PAGES = 4
 HEAD = 256
 VECTOR_COLUMNS = 176
 CLEAR = 256
@@ -47,10 +47,10 @@ def tile_list_embg_dl_none_kernel(tc, dy, w4_words, w4_scales, wd, wgo, offs, ou
         weights = keep.tile([P, J], F32, name="weights")
         pages = [keep.tile([P, T], F32, name="page0")]
 
-        def load(name, src, c0, c1):
+        def load(name, src, c0, c1, tag=""):
             raw = keep.tile([P, PACK, c1 - c0], F32, name="%s_raw%d" % (name, c0), align_bytes=64)
             nc.sync.dma_start(out=raw[:], in_=src[:, c0:c1].rearrange("(p t) c -> p t c", t=PACK))
-            grouped = keep.tile([P, c1 - c0, PACK], BF16, name="%s_bf%d" % (name, c0), align_bytes=64)
+            grouped = keep.tile([P, c1 - c0, PACK], BF16, name="%s_bf%d" % (name, c0), tag=tag or "%s_bf%d" % (name, c0), align_bytes=64)
             return raw, grouped, c0, c1
 
         def weave(piece, copy, lo, hi):
@@ -117,19 +117,21 @@ def tile_list_embg_dl_none_kernel(tc, dy, w4_words, w4_scales, wd, wgo, offs, ou
         words_hbm = w4_words[0].bitcast(I32)
         words_sbuf = w4_codes[:].bitcast(I32)
         dy_a = load("dy", dy, 0, HEAD)
-        nc.sync.dma_start(out=words_sbuf[:, :W4_FIRST], in_=words_hbm[:, :W4_FIRST])
         wd0 = load("wd", wd, 0, P)
+        nc.sync.dma_start(out=words_sbuf[:, :W4_FIRST], in_=words_hbm[:, :W4_FIRST])
         for q in range(QUADRANTS):
             nc.sync.dma_start(out=w4_plane[32 * q : 32 * q + 4, :].bitcast(I32),
                               in_=w4_scales[0, 4 * q : 4 * q + 4, :].bitcast(I32))
         dy_b = load("dy", dy, HEAD, BANK)
         nc.sync.dma_start(offsets[:], offs)
-        nc.sync.dma_start(out=weights[:, :BANK], in_=wgo[:, :BANK])
-        wd12 = load("wd", wd, P, 3 * P)
+        nc.sync.dma_start(out=weights[:, :HEAD], in_=wgo[:, :HEAD])
+        wd1 = load("wd", wd, P, 2 * P, "wd_ring")
+        nc.sync.dma_start(out=weights[:, HEAD:BANK], in_=wgo[:, HEAD:BANK])
+        wd2 = load("wd", wd, 2 * P, 3 * P, "wd_ring")
         nc.sync.dma_start(out=words_sbuf[:, W4_FIRST:], in_=words_hbm[:, W4_FIRST:])
+        wd3 = load("wd", wd, 3 * P, 4 * P, "wd_ring")
         dy_c = load("dy", dy, BANK, J)
         nc.sync.dma_start(out=weights[:, BANK:], in_=wgo[:, BANK:])
-        wd3 = load("wd", wd, 3 * P, 4 * P)
         wd47 = load("wd", wd, 4 * P, N)
 
         weave_on_both(dy_a)
@@ -142,21 +144,27 @@ def tile_list_embg_dl_none_kernel(tc, dy, w4_words, w4_scales, wd, wgo, offs, ou
         place(0, 0, HEAD, "dy_raw256", padded)
         clear_on_gpsimd("dy_bf256")
 
-        weave_on_scalar(wd12)
-        quantise_wd(wd12)
-        clear_on_gpsimd("wd_bf128")
+        weave_on_scalar(wd1)
+        quantise_wd(wd1)
         place(0, HEAD, BANK, "wd_raw128", multiply(0, 0))
-        place(1, 0, BANK, "sums1a", multiply(1, 0))
+        clear_on_gpsimd("wd_raw128")
+        weave_on_scalar(wd2)
+        quantise_wd(wd2)
+        place(1, 0, BANK, "wd_raw256", multiply(1, 0))
+        weave_on_scalar(wd3)
+        quantise_wd(wd3)
+        clear_on_gpsimd("wd_ring")
+        place(2, 0, BANK, "wd_raw384", multiply(2, 0))
         weave_on_scalar(dy_c)
         quantise_dy(dy_c)
-        place(2, 0, BANK, "dy_raw512", multiply(2, 0))
+        place(3, 0, BANK, "dy_raw512", multiply(3, 0))
 
         place(0, BANK, J, "sums0c", multiply(0, BANK))
-        for piece in (wd3, wd47):
-            weave_on_scalar(piece)
-            quantise_wd(piece)
-        place(1, BANK, J, "wd_raw512", multiply(1, BANK))
-        place(2, BANK, J, "sums2b", multiply(2, BANK))
+        place(1, BANK, J, "sums1c", multiply(1, BANK))
+        weave_on_scalar(wd47)
+        quantise_wd(wd47)
+        place(2, BANK, J, "wd_raw512", multiply(2, BANK))
+        place(3, BANK, J, "sums3c", multiply(3, BANK))
 
         for b in range(PAGES, BLOCKS):
             place(b, 0, J, "sums%d" % b, multiply(b, 0) + multiply(b, BANK))

@@ -23,7 +23,7 @@ PSUM_BANKS = 8
 QUADRANTS = 4
 LIST_ROWS = 16
 BLOCKS = N // P
-PAGES = 4
+PAGES = 3
 HEAD = 256
 VECTOR_COLUMNS = 176
 CLEAR = 256
@@ -45,7 +45,7 @@ def tile_list_embg_dl_none_kernel(tc, dy, w4_words, w4_scales, wd, wgo, offs, ou
         dy_codes = keep.tile([P, HEAD + J], U32, name="dy_codes", align_bytes=64)
         dy_plane = keep.tile([P, HEAD + J], U8, name="dy_plane", align_bytes=64)
         weights = keep.tile([P, J], F32, name="weights")
-        pages = [keep.tile([P, T], F32, name="page0")]
+        pages = [keep.tile([P, T], F32, name="page%d" % i) for i in range(PAGES - 1)]
 
         def load(name, src, c0, c1, tag=""):
             raw = keep.tile([P, PACK, c1 - c0], F32, name="%s_raw%d" % (name, c0), align_bytes=64)
@@ -112,7 +112,8 @@ def tile_list_embg_dl_none_kernel(tc, dy, w4_words, w4_scales, wd, wgo, offs, ou
         nc.vector.memset(w4_plane[:].bitcast(U32), 0)
         nc.vector.memset(dy_codes[:, :HEAD], 0)
         nc.vector.memset(dy_plane[:, :HEAD].bitcast(U32), 0)
-        nc.vector.memset(pages[0][:], 0.0)
+        for page in pages:
+            nc.vector.memset(page[:], 0.0)
 
         words_hbm = w4_words[0].bitcast(I32)
         words_sbuf = w4_codes[:].bitcast(I32)
@@ -122,16 +123,16 @@ def tile_list_embg_dl_none_kernel(tc, dy, w4_words, w4_scales, wd, wgo, offs, ou
         for q in range(QUADRANTS):
             nc.sync.dma_start(out=w4_plane[32 * q : 32 * q + 4, :].bitcast(I32),
                               in_=w4_scales[0, 4 * q : 4 * q + 4, :].bitcast(I32))
-        dy_b = load("dy", dy, HEAD, BANK)
+        dy_b = load("dy", dy, HEAD, BANK, "ring")
         nc.sync.dma_start(offsets[:], offs)
         nc.sync.dma_start(out=weights[:, :HEAD], in_=wgo[:, :HEAD])
-        wd1 = load("wd", wd, P, 2 * P, "wd_ring")
+        wd1 = load("wd", wd, P, 2 * P, "ring")
         nc.sync.dma_start(out=weights[:, HEAD:BANK], in_=wgo[:, HEAD:BANK])
-        wd2 = load("wd", wd, 2 * P, 3 * P, "wd_ring")
+        wd2 = load("wd", wd, 2 * P, 3 * P, "ring")
+        dy_c = load("dy", dy, BANK, J, "ring")
         nc.sync.dma_start(out=words_sbuf[:, W4_FIRST:], in_=words_hbm[:, W4_FIRST:])
-        wd3 = load("wd", wd, 3 * P, 4 * P, "wd_ring")
-        dy_c = load("dy", dy, BANK, J)
         nc.sync.dma_start(out=weights[:, BANK:], in_=wgo[:, BANK:])
+        wd3 = load("wd", wd, 3 * P, 4 * P, "ring")
         wd47 = load("wd", wd, 4 * P, N)
 
         weave_on_both(dy_a)
@@ -142,7 +143,6 @@ def tile_list_embg_dl_none_kernel(tc, dy, w4_words, w4_scales, wd, wgo, offs, ou
         weave_on_both(dy_b)
         quantise_dy(dy_b)
         place(0, 0, HEAD, "dy_raw256", padded)
-        clear_on_gpsimd("dy_bf256")
 
         weave_on_scalar(wd1)
         quantise_wd(wd1)
@@ -151,20 +151,16 @@ def tile_list_embg_dl_none_kernel(tc, dy, w4_words, w4_scales, wd, wgo, offs, ou
         weave_on_scalar(wd2)
         quantise_wd(wd2)
         place(1, 0, BANK, "wd_raw256", multiply(1, 0))
-        weave_on_scalar(wd3)
-        quantise_wd(wd3)
-        clear_on_gpsimd("wd_ring")
-        place(2, 0, BANK, "wd_raw384", multiply(2, 0))
         weave_on_scalar(dy_c)
         quantise_dy(dy_c)
-        place(3, 0, BANK, "dy_raw512", multiply(3, 0))
+        place(2, 0, BANK, "dy_raw512", multiply(2, 0))
 
         place(0, BANK, J, "sums0c", multiply(0, BANK))
-        place(1, BANK, J, "sums1c", multiply(1, BANK))
-        weave_on_scalar(wd47)
-        quantise_wd(wd47)
-        place(2, BANK, J, "wd_raw512", multiply(2, BANK))
-        place(3, BANK, J, "sums3c", multiply(3, BANK))
+        for piece in (wd3, wd47):
+            weave_on_scalar(piece)
+            quantise_wd(piece)
+        place(1, BANK, J, "wd_raw512", multiply(1, BANK))
+        place(2, BANK, J, "sums2c", multiply(2, BANK))
 
         for b in range(PAGES, BLOCKS):
             place(b, 0, J, "sums%d" % b, multiply(b, 0) + multiply(b, BANK))

@@ -47,38 +47,41 @@ def tile_list_embg_dl_none_kernel(tc, dy, w4_words, w4_scales, wd, wgo, offs, ou
         weights = keep.tile([P, J], F32, name="weights")
         pages = [keep.tile([P, T], F32, name="page%d" % i) for i in range(PAGES - 1)]
 
-        def load(name, src, c0, c1, tag=""):
-            raw = keep.tile([P, PACK, c1 - c0], F32, name="%s_raw%d" % (name, c0), align_bytes=64)
-            nc.sync.dma_start(out=raw[:], in_=src[:, c0:c1].rearrange("(p t) c -> p t c", t=PACK))
-            grouped = keep.tile([P, c1 - c0, PACK], BF16, name="%s_bf%d" % (name, c0), tag=tag or "%s_bf%d" % (name, c0), align_bytes=64)
-            return raw, grouped, c0, c1
+        def load(name, src, c0, c1, flat=None):
+            if flat is None:
+                flat = keep.tile([P, PACK * (c1 - c0)], F32, name="%s_raw%d" % (name, c0), align_bytes=64)
+            raw = flat[:, : PACK * (c1 - c0)].rearrange("p (t c) -> p t c", t=PACK)
+            nc.sync.dma_start(out=raw, in_=src[:, c0:c1].rearrange("(p t) c -> p t c", t=PACK))
+            return raw
 
-        def weave(piece, copy, lo, hi):
-            raw, grouped = piece[:2]
-            copy(out=grouped[:, lo:hi, :], in_=raw[:, :, lo:hi].rearrange("p t c -> p c t"))
+        def stage(width, tag):
+            return keep.tile([P, width, PACK], BF16, name="grouped", tag=tag, align_bytes=64)
 
-        def weave_on_scalar(piece):
-            for lo in range(0, piece[3] - piece[2], CHUNK):
-                weave(piece, nc.scalar.copy, lo, lo + CHUNK)
+        def weave(copy, raw, grouped, lo, hi):
+            copy(out=grouped[:, lo:hi, :].rearrange("p (c i) t -> p c t i", i=PACK),
+                 in_=raw[:, :, lo:hi].rearrange("p t (c i) -> p c t i", i=PACK))
 
-        def weave_on_both(piece):
-            width = piece[3] - piece[2]
-            cut = width * VECTOR_COLUMNS // HEAD
-            weave(piece, nc.vector.tensor_copy, 0, cut)
-            weave(piece, nc.scalar.copy, cut, width)
+        def weave_on_scalar(raw, grouped):
+            for lo in range(0, raw.shape[2], CHUNK):
+                weave(nc.scalar.copy, raw, grouped, lo, lo + CHUNK)
 
-        def quantise(piece, codes, plane, fmt):
-            grouped = piece[1]
-            nc.vector.quantize_mx(out=codes.bitcast(fmt), scales=plane, in_=grouped[:].rearrange("p c t -> p (c t)"))
+        def weave_on_both(raw, grouped, share=VECTOR_COLUMNS):
+            width = raw.shape[2]
+            cut = width * share // HEAD
+            weave(nc.vector.tensor_copy, raw, grouped, 0, cut)
+            weave(nc.scalar.copy, raw, grouped, cut, width)
 
-        def quantise_dy(piece):
-            cols = slice(HEAD + piece[2], HEAD + piece[3])
-            quantise(piece, dy_codes[:, cols], dy_plane[:, cols], E5M2)
+        def quantise(grouped, codes, plane, fmt):
+            nc.vector.quantize_mx(out=codes.bitcast(fmt), scales=plane, in_=grouped.rearrange("p c t -> p (c t)"))
 
-        def quantise_wd(piece):
-            c0, c1 = piece[2:]
+        def quantise_dy(grouped, c0):
+            cols = slice(HEAD + c0, HEAD + c0 + grouped.shape[1])
+            quantise(grouped, dy_codes[:, cols], dy_plane[:, cols], E5M2)
+
+        def quantise_wd(grouped, c0):
+            c1 = c0 + grouped.shape[1]
             codes = keep.tile([P, c1 - c0], U32, name="wd_codes%d" % c0, align_bytes=64)
-            quantise(piece, codes[:], wd_plane[:, c0:c1], E4M3)
+            quantise(grouped, codes[:], wd_plane[:, c0:c1], E4M3)
             wd_codes.update({b: codes[:, b * P - c0 : (b + 1) * P - c0] for b in range(c0 // P, c1 // P)})
 
         def multiply(b, first):
@@ -94,12 +97,12 @@ def tile_list_embg_dl_none_kernel(tc, dy, w4_words, w4_scales, wd, wgo, offs, ou
             return [(first, acc)]
 
         def place(b, c0, c1, tag, banks):
-            sums = keep.tile([P, c1 - c0], F32, name="sums", tag=tag, align_bytes=64)
+            sums = keep.tile([P, c1 - c0], F32, name="sums", tag=tag, align_bytes=64)[:] if isinstance(tag, str) else tag
             for first, acc in banks:
                 lo, hi = max(first, c0), min(first + BANK, c1)
                 nc.scalar.copy(out=sums[:, lo - c0 : hi - c0], in_=acc[:, lo - first : hi - first])
             window = pages[b % PAGES][:].indirect(offsets[:, c0 // LIST_ROWS : c1 // LIST_ROWS])
-            nc.vector.tensor_tensor(window, sums[:], weights[:, c0:c1], MULT)
+            nc.vector.tensor_tensor(window, sums, weights[:, c0:c1], MULT)
             if c1 == J:
                 nc.sync.dma_start(out=out[b * P : (b + 1) * P, :], in_=pages[b % PAGES][:])
 
@@ -112,8 +115,9 @@ def tile_list_embg_dl_none_kernel(tc, dy, w4_words, w4_scales, wd, wgo, offs, ou
         nc.vector.memset(w4_plane[:].bitcast(U32), 0)
         nc.vector.memset(dy_codes[:, :HEAD], 0)
         nc.vector.memset(dy_plane[:, :HEAD].bitcast(U32), 0)
-        for page in pages:
-            nc.vector.memset(page[:], 0.0)
+        nc.vector.memset(pages[0][:, : T // 2 - 1].bitcast(U32), 0)
+        nc.vector.memset(pages[0][:, T // 2 - 1 :].bitcast(U32), 0)
+        nc.gpsimd.memset(pages[1][:], 0.0)
 
         words_hbm = w4_words[0].bitcast(I32)
         words_sbuf = w4_codes[:].bitcast(I32)
@@ -123,42 +127,53 @@ def tile_list_embg_dl_none_kernel(tc, dy, w4_words, w4_scales, wd, wgo, offs, ou
         for q in range(QUADRANTS):
             nc.sync.dma_start(out=w4_plane[32 * q : 32 * q + 4, :].bitcast(I32),
                               in_=w4_scales[0, 4 * q : 4 * q + 4, :].bitcast(I32))
-        dy_b = load("dy", dy, HEAD, BANK, "ring")
+        shared = keep.tile([P, PACK * HEAD + HEAD - 32], F32, name="shared", align_bytes=64)
+        dy_b = load("dy", dy, HEAD, BANK, shared)
         nc.sync.dma_start(offsets[:], offs)
         nc.sync.dma_start(out=weights[:, :HEAD], in_=wgo[:, :HEAD])
-        wd1 = load("wd", wd, P, 2 * P, "ring")
+        wd1 = load("wd", wd, P, 2 * P)
         nc.sync.dma_start(out=weights[:, HEAD:BANK], in_=wgo[:, HEAD:BANK])
-        wd2 = load("wd", wd, 2 * P, 3 * P, "ring")
-        dy_c = load("dy", dy, BANK, J, "ring")
+        wd2 = load("wd", wd, 2 * P, 3 * P)
+        dy_c = load("dy", dy, BANK, J)
         nc.sync.dma_start(out=words_sbuf[:, W4_FIRST:], in_=words_hbm[:, W4_FIRST:])
         nc.sync.dma_start(out=weights[:, BANK:], in_=wgo[:, BANK:])
-        wd3 = load("wd", wd, 3 * P, 4 * P, "ring")
+        wd3 = load("wd", wd, 3 * P, 4 * P)
         wd47 = load("wd", wd, 4 * P, N)
 
-        weave_on_both(dy_a)
-        quantise_dy(dy_a)
-        weave_on_both(wd0)
-        quantise_wd(wd0)
+        grouped = stage(HEAD, "first")
+        weave_on_both(dy_a, grouped)
+        quantise_dy(grouped[:], 0)
+        grouped = stage(P, "second")
+        weave_on_both(wd0, grouped)
+        quantise_wd(grouped[:], 0)
         padded = multiply(0, -HEAD)
-        weave_on_both(dy_b)
-        quantise_dy(dy_b)
-        place(0, 0, HEAD, "dy_raw256", padded)
+        idle = psum.tile([P, BANK], F32, name="acc")
+        nc.tensor.matmul_mx(out=idle[:], lhsT=wd_codes[0].bitcast(E4M3), lhsT_scale=wd_plane[:, :P],
+                            rhs=dy_codes[:, :BANK].bitcast(E5M2), rhs_scale=dy_plane[:, :BANK], start=True, stop=True)
+        grouped = stage(BANK - HEAD, "third")
+        weave_on_both(dy_b, grouped, 192)
+        quantise_dy(grouped[:], HEAD)
+        place(0, 0, HEAD, shared[:, PACK * HEAD - 32 :], padded)
 
-        weave_on_scalar(wd1)
-        quantise_wd(wd1)
+        grouped = stage(P, "ring")
+        weave_on_scalar(wd1, grouped)
+        quantise_wd(grouped[:], P)
         place(0, HEAD, BANK, "wd_raw128", multiply(0, 0))
         clear_on_gpsimd("wd_raw128")
-        weave_on_scalar(wd2)
-        quantise_wd(wd2)
+        grouped = stage(P, "ring")
+        weave_on_scalar(wd2, grouped)
+        quantise_wd(grouped[:], 2 * P)
         place(1, 0, BANK, "wd_raw256", multiply(1, 0))
-        weave_on_scalar(dy_c)
-        quantise_dy(dy_c)
+        grouped = stage(BANK, "ring")
+        weave_on_scalar(dy_c, grouped)
+        quantise_dy(grouped[:], BANK)
         place(2, 0, BANK, "dy_raw512", multiply(2, 0))
 
         place(0, BANK, J, "sums0c", multiply(0, BANK))
-        for piece in (wd3, wd47):
-            weave_on_scalar(piece)
-            quantise_wd(piece)
+        for raw, c0, tag in ((wd3, 3 * P, "ring"), (wd47, 4 * P, "last")):
+            grouped = stage(raw.shape[2], tag)
+            weave_on_scalar(raw, grouped)
+            quantise_wd(grouped[:], c0)
         place(1, BANK, J, "wd_raw512", multiply(1, BANK))
         place(2, BANK, J, "sums2c", multiply(2, BANK))
 

@@ -115,9 +115,8 @@ def tile_list_embg_dl_none_kernel(tc, dy, w4_words, w4_scales, wd, wgo, offs, ou
         nc.vector.memset(w4_plane[:].bitcast(U32), 0)
         nc.vector.memset(dy_codes[:, :HEAD], 0)
         nc.vector.memset(dy_plane[:, :HEAD].bitcast(U32), 0)
-        nc.vector.memset(pages[0][:, : T // 2 - 1].bitcast(U32), 0)
-        nc.vector.memset(pages[0][:, T // 2 - 1 :].bitcast(U32), 0)
-        nc.gpsimd.memset(pages[1][:], 0.0)
+        for page in pages:
+            nc.vector.memset(page[:], 0.0)
 
         words_hbm = w4_words[0].bitcast(I32)
         words_sbuf = w4_codes[:].bitcast(I32)
@@ -147,11 +146,10 @@ def tile_list_embg_dl_none_kernel(tc, dy, w4_words, w4_scales, wd, wgo, offs, ou
         weave_on_both(wd0, grouped)
         quantise_wd(grouped[:], 0)
         padded = multiply(0, -HEAD)
-        idle = psum.tile([P, BANK], F32, name="acc")
-        nc.tensor.matmul_mx(out=idle[:], lhsT=wd_codes[0].bitcast(E4M3), lhsT_scale=wd_plane[:, :P],
-                            rhs=dy_codes[:, :BANK].bitcast(E5M2), rhs_scale=dy_plane[:, :BANK], start=True, stop=True)
         grouped = stage(BANK - HEAD, "third")
-        weave_on_both(dy_b, grouped, 192)
+        weave(nc.vector.tensor_copy, dy_b, grouped, HEAD - 32, HEAD)
+        weave(nc.scalar.copy, dy_b, grouped, 0, 80)
+        weave(nc.vector.tensor_copy, dy_b, grouped, 80, HEAD - 32)
         quantise_dy(grouped[:], HEAD)
         place(0, 0, HEAD, shared[:, PACK * HEAD - 32 :], padded)
 

@@ -18,6 +18,7 @@ MULT = mybir.AluOpType.mult
 
 P = 128
 PACK = 4
+LINE = 4
 BANK = 512
 PSUM_BANKS = 8
 QUADRANTS = 4
@@ -25,10 +26,11 @@ LIST_ROWS = 16
 BLOCKS = N // P
 PAGES = 3
 HEAD = 256
-VECTOR_COLUMNS = 176
+SCALAR_COLUMNS = 80
+LEAD = 32
 CLEAR = 256
 CHUNK = 128
-W4_FIRST = 2 * P // 2
+EARLY_BLOCKS = 2
 
 
 def tile_list_embg_dl_none_kernel(tc, dy, w4_words, w4_scales, wd, wgo, offs, out):
@@ -47,32 +49,45 @@ def tile_list_embg_dl_none_kernel(tc, dy, w4_words, w4_scales, wd, wgo, offs, ou
         weights = keep.tile([P, J], F32, name="weights")
         pages = [keep.tile([P, T], F32, name="page%d" % i) for i in range(PAGES - 1)]
 
-        def load(name, src, c0, c1, flat=None):
-            if flat is None:
-                flat = keep.tile([P, PACK * (c1 - c0)], F32, name="%s_raw%d" % (name, c0), align_bytes=64)
+        def buffer(columns, tag):
+            return keep.tile([P, columns], F32, name=tag, tag=tag, align_bytes=64)
+
+        def load(src, c0, c1, flat):
             raw = flat[:, : PACK * (c1 - c0)].rearrange("p (t c) -> p t c", t=PACK)
             nc.sync.dma_start(out=raw, in_=src[:, c0:c1].rearrange("(p t) c -> p t c", t=PACK))
             return raw
 
-        def stage(width, tag):
-            return keep.tile([P, width, PACK], BF16, name="grouped", tag=tag, align_bytes=64)
+        def load_own(src, c0, c1, tag):
+            return load(src, c0, c1, buffer(PACK * (c1 - c0), tag))
+
+        def load_w4_scales(c0, c1):
+            for q in range(QUADRANTS):
+                nc.sync.dma_start(out=w4_plane[32 * q : 32 * q + 4, c0:c1].bitcast(I32),
+                                  in_=w4_scales[0, 4 * q : 4 * q + 4, c0:c1].bitcast(I32))
+
+        def rounded(columns, tag):
+            return keep.tile([P, columns, PACK], BF16, name="rounded", tag=tag, align_bytes=64)
 
         def weave(copy, raw, grouped, lo, hi):
-            copy(out=grouped[:, lo:hi, :].rearrange("p (c i) t -> p c t i", i=PACK),
-                 in_=raw[:, :, lo:hi].rearrange("p t (c i) -> p c t i", i=PACK))
+            copy(out=grouped[:, lo:hi, :].rearrange("p (c i) t -> p c t i", i=LINE),
+                 in_=raw[:, :, lo:hi].rearrange("p t (c i) -> p c t i", i=LINE))
 
-        def weave_on_scalar(raw, grouped):
-            for lo in range(0, raw.shape[2], CHUNK):
-                weave(nc.scalar.copy, raw, grouped, lo, lo + CHUNK)
-
-        def weave_on_both(raw, grouped, share=VECTOR_COLUMNS):
+        def weave_on_both(raw, tag):
             width = raw.shape[2]
-            cut = width * share // HEAD
+            cut = width - width * SCALAR_COLUMNS // HEAD
+            grouped = rounded(width, tag)
             weave(nc.vector.tensor_copy, raw, grouped, 0, cut)
             weave(nc.scalar.copy, raw, grouped, cut, width)
+            return grouped
+
+        def weave_on_scalar(raw, tag):
+            grouped = rounded(raw.shape[2], tag)
+            for lo in range(0, raw.shape[2], CHUNK):
+                weave(nc.scalar.copy, raw, grouped, lo, lo + CHUNK)
+            return grouped
 
         def quantise(grouped, codes, plane, fmt):
-            nc.vector.quantize_mx(out=codes.bitcast(fmt), scales=plane, in_=grouped.rearrange("p c t -> p (c t)"))
+            nc.vector.quantize_mx(out=codes.bitcast(fmt), scales=plane, in_=grouped[:].rearrange("p c t -> p (c t)"))
 
         def quantise_dy(grouped, c0):
             cols = slice(HEAD + c0, HEAD + c0 + grouped.shape[1])
@@ -96,8 +111,7 @@ def tile_list_embg_dl_none_kernel(tc, dy, w4_words, w4_scales, wd, wgo, offs, ou
                                 rhs=moving, rhs_scale=dy_plane[:, cols], start=False, stop=True)
             return [(first, acc)]
 
-        def place(b, c0, c1, tag, banks):
-            sums = keep.tile([P, c1 - c0], F32, name="sums", tag=tag, align_bytes=64)[:] if isinstance(tag, str) else tag
+        def place(b, c0, c1, banks, sums):
             for first, acc in banks:
                 lo, hi = max(first, c0), min(first + BANK, c1)
                 nc.scalar.copy(out=sums[:, lo - c0 : hi - c0], in_=acc[:, lo - first : hi - first])
@@ -105,12 +119,6 @@ def tile_list_embg_dl_none_kernel(tc, dy, w4_words, w4_scales, wd, wgo, offs, ou
             nc.vector.tensor_tensor(window, sums, weights[:, c0:c1], MULT)
             if c1 == J:
                 nc.sync.dma_start(out=out[b * P : (b + 1) * P, :], in_=pages[b % PAGES][:])
-
-        def clear_on_gpsimd(tag):
-            page = keep.tile([P, T], F32, name="page", tag=tag, align_bytes=64)
-            pages.append(page)
-            for lo in range(0, T, CLEAR):
-                nc.gpsimd.memset(page[:, lo : lo + CLEAR], 0.0)
 
         nc.vector.memset(w4_plane[:].bitcast(U32), 0)
         nc.vector.memset(dy_codes[:, :HEAD], 0)
@@ -120,60 +128,51 @@ def tile_list_embg_dl_none_kernel(tc, dy, w4_words, w4_scales, wd, wgo, offs, ou
 
         words_hbm = w4_words[0].bitcast(I32)
         words_sbuf = w4_codes[:].bitcast(I32)
-        dy_a = load("dy", dy, 0, HEAD)
-        wd0 = load("wd", wd, 0, P)
-        nc.sync.dma_start(out=words_sbuf[:, :W4_FIRST], in_=words_hbm[:, :W4_FIRST])
-        for q in range(QUADRANTS):
-            nc.sync.dma_start(out=w4_plane[32 * q : 32 * q + 4, :].bitcast(I32),
-                              in_=w4_scales[0, 4 * q : 4 * q + 4, :].bitcast(I32))
-        shared = keep.tile([P, PACK * HEAD + HEAD - 32], F32, name="shared", align_bytes=64)
-        dy_b = load("dy", dy, HEAD, BANK, shared)
+        early_words = EARLY_BLOCKS * P // 2
+        dy_a = load_own(dy, 0, HEAD, "dy_a")
+        wd_0 = load_own(wd, 0, P, "wd_0")
+        nc.sync.dma_start(out=words_sbuf[:, :early_words], in_=words_hbm[:, :early_words])
+        load_w4_scales(0, PAGES * P)
+        dy_b_and_sums = buffer(PACK * (BANK - HEAD) - LEAD + HEAD, "dy_b_and_sums")
+        dy_b = load(dy, HEAD, BANK, dy_b_and_sums)
         nc.sync.dma_start(offsets[:], offs)
         nc.sync.dma_start(out=weights[:, :HEAD], in_=wgo[:, :HEAD])
-        wd1 = load("wd", wd, P, 2 * P)
+        wd_1 = load_own(wd, P, 2 * P, "wd_1")
         nc.sync.dma_start(out=weights[:, HEAD:BANK], in_=wgo[:, HEAD:BANK])
-        wd2 = load("wd", wd, 2 * P, 3 * P)
-        dy_c = load("dy", dy, BANK, J)
-        nc.sync.dma_start(out=words_sbuf[:, W4_FIRST:], in_=words_hbm[:, W4_FIRST:])
+        wd_2 = load_own(wd, 2 * P, 3 * P, "wd_2")
+        dy_c = load_own(dy, BANK, J, "dy_c")
+        nc.sync.dma_start(out=words_sbuf[:, early_words:], in_=words_hbm[:, early_words:])
         nc.sync.dma_start(out=weights[:, BANK:], in_=wgo[:, BANK:])
-        wd3 = load("wd", wd, 3 * P, 4 * P)
-        wd47 = load("wd", wd, 4 * P, N)
+        wd_3 = load_own(wd, 3 * P, 4 * P, "wd_3")
+        wd_47 = load_own(wd, 4 * P, N, "wd_47")
+        load_w4_scales(PAGES * P, N)
 
-        grouped = stage(HEAD, "first")
-        weave_on_both(dy_a, grouped)
-        quantise_dy(grouped[:], 0)
-        grouped = stage(P, "second")
-        weave_on_both(wd0, grouped)
-        quantise_wd(grouped[:], 0)
+        quantise_dy(weave_on_both(dy_a, "rounded_dy_a"), 0)
+        quantise_wd(weave_on_both(wd_0, "rounded_wd_0"), 0)
         padded = multiply(0, -HEAD)
-        grouped = stage(BANK - HEAD, "third")
-        weave(nc.vector.tensor_copy, dy_b, grouped, HEAD - 32, HEAD)
-        weave(nc.scalar.copy, dy_b, grouped, 0, 80)
-        weave(nc.vector.tensor_copy, dy_b, grouped, 80, HEAD - 32)
-        quantise_dy(grouped[:], HEAD)
-        place(0, 0, HEAD, shared[:, PACK * HEAD - 32 :], padded)
+        width = BANK - HEAD
+        grouped = rounded(width, "rounded_dy_b")
+        weave(nc.vector.tensor_copy, dy_b, grouped, width - LEAD, width)
+        weave(nc.scalar.copy, dy_b, grouped, 0, SCALAR_COLUMNS)
+        weave(nc.vector.tensor_copy, dy_b, grouped, SCALAR_COLUMNS, width - LEAD)
+        quantise_dy(grouped, HEAD)
+        place(0, 0, HEAD, padded, dy_b_and_sums[:, PACK * width - LEAD :])
 
-        grouped = stage(P, "ring")
-        weave_on_scalar(wd1, grouped)
-        quantise_wd(grouped[:], P)
-        place(0, HEAD, BANK, "wd_raw128", multiply(0, 0))
-        clear_on_gpsimd("wd_raw128")
-        grouped = stage(P, "ring")
-        weave_on_scalar(wd2, grouped)
-        quantise_wd(grouped[:], 2 * P)
-        place(1, 0, BANK, "wd_raw256", multiply(1, 0))
-        grouped = stage(BANK, "ring")
-        weave_on_scalar(dy_c, grouped)
-        quantise_dy(grouped[:], BANK)
-        place(2, 0, BANK, "dy_raw512", multiply(2, 0))
+        quantise_wd(weave_on_scalar(wd_1, "ring"), P)
+        place(0, HEAD, BANK, multiply(0, 0), buffer(BANK - HEAD, "wd_1")[:])
+        pages.append(buffer(T, "wd_1"))
+        for lo in range(0, T, CLEAR):
+            nc.gpsimd.memset(pages[-1][:, lo : lo + CLEAR], 0.0)
+        quantise_wd(weave_on_scalar(wd_2, "ring"), 2 * P)
+        place(1, 0, BANK, multiply(1, 0), buffer(BANK, "wd_2")[:])
+        quantise_dy(weave_on_scalar(dy_c, "ring"), BANK)
+        place(2, 0, BANK, multiply(2, 0), buffer(BANK, "dy_c")[:])
 
-        place(0, BANK, J, "sums0c", multiply(0, BANK))
-        for raw, c0, tag in ((wd3, 3 * P, "ring"), (wd47, 4 * P, "last")):
-            grouped = stage(raw.shape[2], tag)
-            weave_on_scalar(raw, grouped)
-            quantise_wd(grouped[:], c0)
-        place(1, BANK, J, "wd_raw512", multiply(1, BANK))
-        place(2, BANK, J, "sums2c", multiply(2, BANK))
+        place(0, BANK, J, multiply(0, BANK), buffer(BANK, "sums_0")[:])
+        quantise_wd(weave_on_scalar(wd_3, "ring"), 3 * P)
+        quantise_wd(weave_on_scalar(wd_47, "rounded_wd_47"), 4 * P)
+        place(1, BANK, J, multiply(1, BANK), buffer(BANK, "wd_47")[:])
+        place(2, BANK, J, multiply(2, BANK), buffer(BANK, "sums_2")[:])
 
         for b in range(PAGES, BLOCKS):
-            place(b, 0, J, "sums%d" % b, multiply(b, 0) + multiply(b, BANK))
+            place(b, 0, J, multiply(b, 0) + multiply(b, BANK), buffer(J, "sums_%d" % b)[:])

@@ -26,11 +26,10 @@ LIST_ROWS = 16
 BLOCKS = N // P
 PAGES = 3
 HEAD = 256
-SCALAR_COLUMNS = 80
+SCALAR_COLUMNS = 96
 LEAD = 32
 CLEAR = 256
 CHUNK = 128
-EARLY_BLOCKS = 2
 
 
 def tile_list_embg_dl_none_kernel(tc, dy, w4_words, w4_scales, wd, wgo, offs, out):
@@ -60,10 +59,14 @@ def tile_list_embg_dl_none_kernel(tc, dy, w4_words, w4_scales, wd, wgo, offs, ou
         def load_own(src, c0, c1, tag):
             return load(src, c0, c1, buffer(PACK * (c1 - c0), tag))
 
-        def load_w4_scales(c0, c1):
+        def load_w4_scales(queue, c0, c1):
             for q in range(QUADRANTS):
-                nc.sync.dma_start(out=w4_plane[32 * q : 32 * q + 4, c0:c1].bitcast(I32),
-                                  in_=w4_scales[0, 4 * q : 4 * q + 4, c0:c1].bitcast(I32))
+                queue.dma_start(out=w4_plane[32 * q : 32 * q + 4, c0:c1].bitcast(I32),
+                                in_=w4_scales[0, 4 * q : 4 * q + 4, c0:c1].bitcast(I32))
+
+        def load_w4_words(queue, b0, b1):
+            cols = slice(b0 * P // 2, b1 * P // 2)
+            queue.dma_start(out=w4_codes[:].bitcast(I32)[:, cols], in_=w4_words[0].bitcast(I32)[:, cols])
 
         def rounded(columns, tag):
             return keep.tile([P, columns, PACK], BF16, name="rounded", tag=tag, align_bytes=64)
@@ -74,7 +77,7 @@ def tile_list_embg_dl_none_kernel(tc, dy, w4_words, w4_scales, wd, wgo, offs, ou
 
         def weave_on_both(raw, tag):
             width = raw.shape[2]
-            cut = width - width * SCALAR_COLUMNS // HEAD
+            cut = width // 2
             grouped = rounded(width, tag)
             weave(nc.vector.tensor_copy, raw, grouped, 0, cut)
             weave(nc.scalar.copy, raw, grouped, cut, width)
@@ -126,29 +129,28 @@ def tile_list_embg_dl_none_kernel(tc, dy, w4_words, w4_scales, wd, wgo, offs, ou
         for page in pages:
             nc.vector.memset(page[:], 0.0)
 
-        words_hbm = w4_words[0].bitcast(I32)
-        words_sbuf = w4_codes[:].bitcast(I32)
-        early_words = EARLY_BLOCKS * P // 2
         dy_a = load_own(dy, 0, HEAD, "dy_a")
         wd_0 = load_own(wd, 0, P, "wd_0")
-        nc.sync.dma_start(out=words_sbuf[:, :early_words], in_=words_hbm[:, :early_words])
-        load_w4_scales(0, PAGES * P)
+        load_w4_words(nc.sync, 0, 1)
+        load_w4_scales(nc.sync, 0, P)
         dy_b_and_sums = buffer(PACK * (BANK - HEAD) - LEAD + HEAD, "dy_b_and_sums")
         dy_b = load(dy, HEAD, BANK, dy_b_and_sums)
         nc.sync.dma_start(offsets[:], offs)
         nc.sync.dma_start(out=weights[:, :HEAD], in_=wgo[:, :HEAD])
         wd_1 = load_own(wd, P, 2 * P, "wd_1")
+        load_w4_words(nc.sync, 1, PAGES)
+        load_w4_scales(nc.sync, P, PAGES * P)
         nc.sync.dma_start(out=weights[:, HEAD:BANK], in_=wgo[:, HEAD:BANK])
         wd_2 = load_own(wd, 2 * P, 3 * P, "wd_2")
         dy_c = load_own(dy, BANK, J, "dy_c")
-        nc.sync.dma_start(out=words_sbuf[:, early_words:], in_=words_hbm[:, early_words:])
+        load_w4_words(nc.sync, PAGES, BLOCKS)
         nc.sync.dma_start(out=weights[:, BANK:], in_=wgo[:, BANK:])
         wd_3 = load_own(wd, 3 * P, 4 * P, "wd_3")
         wd_47 = load_own(wd, 4 * P, N, "wd_47")
-        load_w4_scales(PAGES * P, N)
+        load_w4_scales(nc.sync, PAGES * P, N)
 
         quantise_dy(weave_on_both(dy_a, "rounded_dy_a"), 0)
-        quantise_wd(weave_on_both(wd_0, "rounded_wd_0"), 0)
+        quantise_wd(weave_on_scalar(wd_0, "rounded_wd_0"), 0)
         padded = multiply(0, -HEAD)
         width = BANK - HEAD
         grouped = rounded(width, "rounded_dy_b")

@@ -142,7 +142,8 @@ def tile_list_embg_dl_none_kernel(tc, dy, w4_words, w4_scales, wd, wgo, offs, ou
         load_w4_scales(nc.sync, P, PAGES * P)
         nc.sync.dma_start(out=weights[:, HEAD:BANK], in_=wgo[:, HEAD:BANK])
         wd_2 = load_own(wd, 2 * P, 3 * P, "wd_2")
-        dy_c = load_own(dy, BANK, J, "dy_c")
+        dy_c = load_own(dy, BANK, BANK + HEAD, "dy_c")
+        dy_d = load_own(dy, BANK + HEAD, J, "dy_d")
         load_w4_words(nc.sync, PAGES, BLOCKS)
         nc.sync.dma_start(out=weights[:, BANK:], in_=wgo[:, BANK:])
         wd_3 = load_own(wd, 3 * P, 4 * P, "wd_3")
@@ -167,8 +168,12 @@ def tile_list_embg_dl_none_kernel(tc, dy, w4_words, w4_scales, wd, wgo, offs, ou
             nc.gpsimd.memset(pages[-1][:, lo : lo + CLEAR], 0.0)
         quantise_wd(weave_on_scalar(wd_2, "ring"), 2 * P)
         place(1, 0, BANK, multiply(1, 0), buffer(BANK, "wd_2")[:])
-        quantise_dy(weave_on_scalar(dy_c, "ring"), BANK)
-        place(2, 0, BANK, multiply(2, 0), buffer(BANK, "dy_c")[:])
+        grouped = rounded(J - BANK, "ring")
+        for first, raw in ((0, dy_c), (HEAD, dy_d)):
+            for lo in range(0, HEAD, CHUNK):
+                weave(nc.scalar.copy, raw, grouped[:, first : first + HEAD, :], lo, lo + CHUNK)
+        quantise_dy(grouped, BANK)
+        place(2, 0, BANK, multiply(2, 0), buffer(BANK, "dy_d")[:])
 
         place(0, BANK, J, multiply(0, BANK), buffer(BANK, "sums_0")[:])
         quantise_wd(weave_on_scalar(wd_3, "ring"), 3 * P)

@@ -138,10 +138,10 @@ def tile_list_embg_dl_none_kernel(tc, dy, w4_words, w4_scales, wd, wgo, offs, ou
         nc.sync.dma_start(offsets[:], offs)
         nc.sync.dma_start(out=weights[:, :HEAD], in_=wgo[:, :HEAD])
         wd_1 = load_own(wd, P, 2 * P, "wd_1")
+        wd_2 = load_own(wd, 2 * P, 3 * P, "wd_2")
+        nc.sync.dma_start(out=weights[:, HEAD:BANK], in_=wgo[:, HEAD:BANK])
         load_w4_words(nc.sync, 1, PAGES)
         load_w4_scales(nc.sync, P, PAGES * P)
-        nc.sync.dma_start(out=weights[:, HEAD:BANK], in_=wgo[:, HEAD:BANK])
-        wd_2 = load_own(wd, 2 * P, 3 * P, "wd_2")
         dy_c = load_own(dy, BANK, BANK + HEAD, "dy_c")
         dy_d = load_own(dy, BANK + HEAD, J, "dy_d")
         load_w4_words(nc.sync, PAGES, BLOCKS)
@@ -161,14 +161,16 @@ def tile_list_embg_dl_none_kernel(tc, dy, w4_words, w4_scales, wd, wgo, offs, ou
         quantise_dy(grouped, HEAD)
         place(0, 0, HEAD, padded, dy_b_and_sums[:, PACK * width - LEAD :])
 
-        quantise_wd(weave_on_scalar(wd_1, "ring"), P)
-        place(0, HEAD, BANK, multiply(0, 0), buffer(BANK - HEAD, "wd_1")[:])
-        pages.append(buffer(T, "wd_1"))
+        grouped = rounded(2 * P, "rounded_wd_12")
+        for first, raw in ((0, wd_1), (P, wd_2)):
+            weave(nc.scalar.copy, raw, grouped[:, first : first + P, :], 0, P)
+        quantise_wd(grouped, P)
+        place(0, HEAD, BANK, multiply(0, 0), buffer(BANK - HEAD, "wd_2")[:])
+        pages.append(buffer(T, "rounded_wd_12"))
         for lo in range(0, T, CLEAR):
             nc.gpsimd.memset(pages[-1][:, lo : lo + CLEAR], 0.0)
-        quantise_wd(weave_on_scalar(wd_2, "ring"), 2 * P)
-        place(1, 0, BANK, multiply(1, 0), buffer(BANK, "wd_2")[:])
-        grouped = rounded(J - BANK, "ring")
+        place(1, 0, BANK, multiply(1, 0), buffer(BANK, "sums_1")[:])
+        grouped = rounded(J - BANK, "wd_2")
         for first, raw in ((0, dy_c), (HEAD, dy_d)):
             for lo in range(0, HEAD, CHUNK):
                 weave(nc.scalar.copy, raw, grouped[:, first : first + HEAD, :], lo, lo + CHUNK)
@@ -176,7 +178,7 @@ def tile_list_embg_dl_none_kernel(tc, dy, w4_words, w4_scales, wd, wgo, offs, ou
         place(2, 0, BANK, multiply(2, 0), buffer(BANK, "dy_d")[:])
 
         place(0, BANK, J, multiply(0, BANK), buffer(BANK, "sums_0")[:])
-        quantise_wd(weave_on_scalar(wd_3, "ring"), 3 * P)
+        quantise_wd(weave_on_scalar(wd_3, "wd_2"), 3 * P)
         quantise_wd(weave_on_scalar(wd_47, "rounded_wd_47"), 4 * P)
         place(1, BANK, J, multiply(1, BANK), buffer(BANK, "wd_47")[:])
         place(2, BANK, J, multiply(2, BANK), buffer(BANK, "sums_2")[:])

@@ -77,7 +77,7 @@ def tile_list_embg_dl_none_kernel(tc, dy, w4_words, w4_scales, wd, wgo, offs, ou
 
         def weave_on_both(raw, tag):
             width = raw.shape[2]
-            cut = width // 2
+            cut = width - SCALAR_COLUMNS
             grouped = rounded(width, tag)
             weave(nc.vector.tensor_copy, raw, grouped, 0, cut)
             weave(nc.scalar.copy, raw, grouped, cut, width)
@@ -132,16 +132,15 @@ def tile_list_embg_dl_none_kernel(tc, dy, w4_words, w4_scales, wd, wgo, offs, ou
         dy_a = load_own(dy, 0, HEAD, "dy_a")
         wd_0 = load_own(wd, 0, P, "wd_0")
         load_w4_words(nc.sync, 0, 1)
-        load_w4_scales(nc.sync, 0, P)
+        load_w4_scales(nc.sync, 0, PAGES * P)
         dy_b_and_sums = buffer(PACK * (BANK - HEAD) - LEAD + HEAD, "dy_b_and_sums")
         dy_b = load(dy, HEAD, BANK, dy_b_and_sums)
         nc.sync.dma_start(offsets[:], offs)
         nc.sync.dma_start(out=weights[:, :HEAD], in_=wgo[:, :HEAD])
         wd_1 = load_own(wd, P, 2 * P, "wd_1")
         wd_2 = load_own(wd, 2 * P, 3 * P, "wd_2")
-        nc.sync.dma_start(out=weights[:, HEAD:BANK], in_=wgo[:, HEAD:BANK])
         load_w4_words(nc.sync, 1, PAGES)
-        load_w4_scales(nc.sync, P, PAGES * P)
+        nc.sync.dma_start(out=weights[:, HEAD:BANK], in_=wgo[:, HEAD:BANK])
         dy_c = load_own(dy, BANK, BANK + HEAD, "dy_c")
         dy_d = load_own(dy, BANK + HEAD, J, "dy_d")
         load_w4_words(nc.sync, PAGES, BLOCKS)

@@ -146,7 +146,8 @@ def tile_list_embg_dl_none_kernel(tc, dy, w4_words, w4_scales, wd, wgo, offs, ou
         load_w4_words(nc.sync, PAGES, BLOCKS)
         nc.sync.dma_start(out=weights[:, BANK:], in_=wgo[:, BANK:])
         wd_3 = load_own(wd, 3 * P, 4 * P, "wd_3")
-        wd_47 = load_own(wd, 4 * P, N, "wd_47")
+        wd_47_and_sums = buffer(PACK * (N - 4 * P), "wd_47")
+        wd_47 = load(wd, 4 * P, N, wd_47_and_sums)
         load_w4_scales(nc.sync, PAGES * P, N)
 
         quantise_dy(weave_on_both(dy_a, "rounded_dy_a"), 0)
@@ -178,9 +179,10 @@ def tile_list_embg_dl_none_kernel(tc, dy, w4_words, w4_scales, wd, wgo, offs, ou
 
         place(0, BANK, J, multiply(0, BANK), buffer(BANK, "sums_0")[:])
         quantise_wd(weave_on_scalar(wd_3, "wd_2"), 3 * P)
-        quantise_wd(weave_on_scalar(wd_47, "rounded_wd_47"), 4 * P)
-        place(1, BANK, J, multiply(1, BANK), buffer(BANK, "wd_47")[:])
+        place(1, BANK, J, multiply(1, BANK), buffer(BANK, "wd_3")[:])
         place(2, BANK, J, multiply(2, BANK), buffer(BANK, "sums_2")[:])
+        quantise_wd(weave_on_scalar(wd_47, "sums_0"), 4 * P)
 
         for b in range(PAGES, BLOCKS):
-            place(b, 0, J, multiply(b, 0) + multiply(b, BANK), buffer(J, "sums_%d" % b)[:])
+            sums = wd_47_and_sums[:, :J] if b == PAGES else buffer(J, "sums_%d" % b)[:]
+            place(b, 0, J, multiply(b, 0) + multiply(b, BANK), sums)

@@ -135,8 +135,8 @@ def tile_list_embg_dl_none_kernel(tc, dy, w4_words, w4_scales, wd, wgo, offs, ou
         load_w4_scales(nc.sync, 0, PAGES * P)
         dy_b_and_sums = buffer(PACK * (BANK - HEAD) - LEAD + HEAD, "dy_b_and_sums")
         dy_b = load(dy, HEAD, BANK, dy_b_and_sums)
-        nc.sync.dma_start(offsets[:], offs)
         nc.sync.dma_start(out=weights[:, :HEAD], in_=wgo[:, :HEAD])
+        nc.sync.dma_start(offsets[:], offs)
         wd_1 = load_own(wd, P, 2 * P, "wd_1")
         wd_2 = load_own(wd, 2 * P, 3 * P, "wd_2")
         load_w4_words(nc.sync, 1, PAGES)

@@ -25,164 +25,150 @@ QUADRANTS = 4
 LIST_ROWS = 16
 BLOCKS = N // P
 PAGES = 3
-HEAD = 256
+EARLY = 2
+PIECES = ((0, 256), (256, 384), (384, 512), (512, 768), (768, 1024))
 SCALAR_COLUMNS = 96
 LEAD = 32
-CLEAR = 256
+CLEAR = 512
 CHUNK = 128
+OVERLAP = 64
+ROUNDED_BYTES = 2 * PACK * P
+RING = {"rounded_dy_1": 0, "rounded_wd_0": ROUNDED_BYTES - OVERLAP, "rounded_wd_1": ROUNDED_BYTES - OVERLAP}
 
 
 def tile_list_embg_dl_none_kernel(tc, dy, w4_words, w4_scales, wd, wgo, offs, out):
     nc = tc.nc
     with ExitStack() as ctx:
         keep = ctx.enter_context(tc.tile_pool(name="keep", bufs=1))
+        ring = ctx.enter_context(tc.tile_pool(name="ring", bufs=1))
         psum = ctx.enter_context(tc.psum_pool(name="psum", bufs=PSUM_BANKS))
 
         offsets = keep.tile([P, J // LIST_ROWS], U16, name="offsets")
         w4_codes = keep.tile([P, 2 * N], U8, name="w4_codes", align_bytes=64)
         w4_plane = keep.tile([P, N], U8, name="w4_plane", align_bytes=64)
-        wd_codes = {}
+        wd_codes = keep.tile([P, N], U32, name="wd_codes", align_bytes=64)
         wd_plane = keep.tile([P, N], U8, name="wd_plane", align_bytes=64)
-        dy_codes = keep.tile([P, HEAD + J], U32, name="dy_codes", align_bytes=64)
-        dy_plane = keep.tile([P, HEAD + J], U8, name="dy_plane", align_bytes=64)
+        dy_codes = keep.tile([P, J], U32, name="dy_codes", align_bytes=64)
+        dy_plane = keep.tile([P, J], U8, name="dy_plane", align_bytes=64)
         weights = keep.tile([P, J], F32, name="weights")
         pages = [keep.tile([P, T], F32, name="page%d" % i) for i in range(PAGES - 1)]
 
         def buffer(columns, tag):
             return keep.tile([P, columns], F32, name=tag, tag=tag, align_bytes=64)
 
-        def load(src, c0, c1, flat):
-            raw = flat[:, : PACK * (c1 - c0)].rearrange("p (t c) -> p t c", t=PACK)
+        def load(src, c0, c1, tag, sums=LEAD):
+            size = PACK * (c1 - c0)
+            flat = buffer(size - LEAD + sums, tag)
+            raw = flat[:, :size].rearrange("p (t c) -> p t c", t=PACK)
             nc.sync.dma_start(out=raw, in_=src[:, c0:c1].rearrange("(p t) c -> p t c", t=PACK))
-            return raw
+            return raw, (flat[:, size - LEAD :], flat[:, :sums])
 
-        def load_own(src, c0, c1, tag):
-            return load(src, c0, c1, buffer(PACK * (c1 - c0), tag))
-
-        def load_w4_scales(queue, c0, c1):
+        def load_w4_scales(c0, c1):
             for q in range(QUADRANTS):
-                queue.dma_start(out=w4_plane[32 * q : 32 * q + 4, c0:c1].bitcast(I32),
-                                in_=w4_scales[0, 4 * q : 4 * q + 4, c0:c1].bitcast(I32))
+                nc.sync.dma_start(out=w4_plane[32 * q : 32 * q + 4, c0:c1].bitcast(I32),
+                                  in_=w4_scales[0, 4 * q : 4 * q + 4, c0:c1].bitcast(I32))
 
-        def load_w4_words(queue, b0, b1):
+        def load_w4_words(b0, b1):
             cols = slice(b0 * P // 2, b1 * P // 2)
-            queue.dma_start(out=w4_codes[:].bitcast(I32)[:, cols], in_=w4_words[0].bitcast(I32)[:, cols])
+            nc.sync.dma_start(out=w4_codes[:].bitcast(I32)[:, cols], in_=w4_words[0].bitcast(I32)[:, cols])
+
+        def load_weights(c0, c1):
+            nc.sync.dma_start(out=weights[:, c0:c1], in_=wgo[:, c0:c1])
 
         def rounded(columns, tag):
+            if tag in RING:
+                return ring.tile([P, columns, PACK], BF16, name=tag, align_bytes=64, offset=RING[tag])
             return keep.tile([P, columns, PACK], BF16, name="rounded", tag=tag, align_bytes=64)
 
         def weave(copy, raw, grouped, lo, hi):
             copy(out=grouped[:, lo:hi, :].rearrange("p (c i) t -> p c t i", i=LINE),
                  in_=raw[:, :, lo:hi].rearrange("p t (c i) -> p c t i", i=LINE))
 
-        def weave_on_both(raw, tag):
+        def weave_lead_first(copy, raw, tag):
             width = raw.shape[2]
-            cut = width - SCALAR_COLUMNS
             grouped = rounded(width, tag)
-            weave(nc.vector.tensor_copy, raw, grouped, 0, cut)
-            weave(nc.scalar.copy, raw, grouped, cut, width)
+            weave(copy, raw, grouped, width - LEAD, width)
+            for lo in range(0, width - LEAD, CHUNK):
+                weave(copy, raw, grouped, lo, min(lo + CHUNK, width - LEAD))
             return grouped
 
-        def weave_on_scalar(raw, tag):
-            grouped = rounded(raw.shape[2], tag)
-            for lo in range(0, raw.shape[2], CHUNK):
-                weave(nc.scalar.copy, raw, grouped, lo, lo + CHUNK)
-            return grouped
+        def quantise(grouped, codes, plane, c0, fmt):
+            cols = slice(c0, c0 + grouped.shape[1])
+            nc.vector.quantize_mx(out=codes[:, cols].bitcast(fmt), scales=plane[:, cols],
+                                  in_=grouped[:].rearrange("p c t -> p (c t)"))
 
-        def quantise(grouped, codes, plane, fmt):
-            nc.vector.quantize_mx(out=codes.bitcast(fmt), scales=plane, in_=grouped[:].rearrange("p c t -> p (c t)"))
-
-        def quantise_dy(grouped, c0):
-            cols = slice(HEAD + c0, HEAD + c0 + grouped.shape[1])
-            quantise(grouped, dy_codes[:, cols], dy_plane[:, cols], E5M2)
-
-        def quantise_wd(grouped, c0):
-            c1 = c0 + grouped.shape[1]
-            codes = keep.tile([P, c1 - c0], U32, name="wd_codes%d" % c0, align_bytes=64)
-            quantise(grouped, codes[:], wd_plane[:, c0:c1], E4M3)
-            wd_codes.update({b: codes[:, b * P - c0 : (b + 1) * P - c0] for b in range(c0 // P, c1 // P)})
-
-        def multiply(b, first):
+        def place(b, c0, c1, sums):
             rows = slice(b * P, (b + 1) * P)
-            cols = slice(HEAD + first, HEAD + first + BANK)
-            acc = psum.tile([P, BANK], F32, name="acc")
-            moving = dy_codes[:, cols].bitcast(E5M2)
-            nc.tensor.matmul_mx(out=acc[:], lhsT=w4_codes[:, 2 * b * P : 2 * (b + 1) * P].bitcast(E2M1),
-                                lhsT_scale=w4_plane[:, rows], rhs=moving, rhs_scale=dy_plane[:, cols],
-                                start=True, stop=False)
-            nc.tensor.matmul_mx(out=acc[:], lhsT=wd_codes[b].bitcast(E4M3), lhsT_scale=wd_plane[:, rows],
-                                rhs=moving, rhs_scale=dy_plane[:, cols], start=False, stop=True)
-            return [(first, acc)]
-
-        def place(b, c0, c1, banks, sums):
-            for first, acc in banks:
-                lo, hi = max(first, c0), min(first + BANK, c1)
-                nc.scalar.copy(out=sums[:, lo - c0 : hi - c0], in_=acc[:, lo - first : hi - first])
+            for lo in range(c0, c1, BANK):
+                hi = min(lo + BANK, c1)
+                acc = psum.tile([P, BANK], F32, name="acc")
+                moving = dy_codes[:, lo:hi].bitcast(E5M2)
+                nc.tensor.matmul_mx(out=acc[:, : hi - lo], lhsT=w4_codes[:, 2 * b * P : 2 * (b + 1) * P].bitcast(E2M1),
+                                    lhsT_scale=w4_plane[:, rows], rhs=moving, rhs_scale=dy_plane[:, lo:hi],
+                                    start=True, stop=False)
+                nc.tensor.matmul_mx(out=acc[:, : hi - lo], lhsT=wd_codes[:, rows].bitcast(E4M3),
+                                    lhsT_scale=wd_plane[:, rows], rhs=moving, rhs_scale=dy_plane[:, lo:hi],
+                                    start=False, stop=True)
+                nc.scalar.copy(out=sums[:, lo - c0 : hi - c0], in_=acc[:, : hi - lo])
             window = pages[b % PAGES][:].indirect(offsets[:, c0 // LIST_ROWS : c1 // LIST_ROWS])
             nc.vector.tensor_tensor(window, sums, weights[:, c0:c1], MULT)
             if c1 == J:
                 nc.sync.dma_start(out=out[b * P : (b + 1) * P, :], in_=pages[b % PAGES][:])
 
-        nc.vector.memset(w4_plane[:].bitcast(U32), 0)
-        nc.vector.memset(dy_codes[:, :HEAD], 0)
-        nc.vector.memset(dy_plane[:, :HEAD].bitcast(U32), 0)
-        for page in pages:
-            nc.vector.memset(page[:], 0.0)
+        def clear_in_odd_halves(view, value):
+            cut = view.shape[1] // 2 - 1
+            nc.vector.memset(view[:, :cut], value)
+            nc.vector.memset(view[:, cut:], value)
 
-        dy_a = load_own(dy, 0, HEAD, "dy_a")
-        wd_0 = load_own(wd, 0, P, "wd_0")
-        load_w4_words(nc.sync, 0, 1)
-        load_w4_scales(nc.sync, 0, PAGES * P)
-        dy_b_and_sums = buffer(PACK * (BANK - HEAD) - LEAD + HEAD, "dy_b_and_sums")
-        dy_b = load(dy, HEAD, BANK, dy_b_and_sums)
-        nc.sync.dma_start(out=weights[:, :HEAD], in_=wgo[:, :HEAD])
+        clear_in_odd_halves(w4_plane[:].bitcast(U32), 0)
+        clear_in_odd_halves(pages[0][:], 0.0)
+        nc.gpsimd.memset(pages[1][:], 0.0)
+
+        width = [c1 - c0 for c0, c1 in PIECES]
+        dy_0, spare = load(dy, *PIECES[0], "dy_0")
+        wd_0, spare = load(wd, 0, P, "wd_0")
+        load_w4_words(0, EARLY)
+        load_w4_scales(0, EARLY * P)
+        wd_1, sums_a = load(wd, P, 2 * P, "wd_1", width[0])
+        load_weights(*PIECES[0])
         nc.sync.dma_start(offsets[:], offs)
-        wd_1 = load_own(wd, P, 2 * P, "wd_1")
-        wd_2 = load_own(wd, 2 * P, 3 * P, "wd_2")
-        load_w4_words(nc.sync, 1, PAGES)
-        nc.sync.dma_start(out=weights[:, HEAD:BANK], in_=wgo[:, HEAD:BANK])
-        dy_c = load_own(dy, BANK, BANK + HEAD, "dy_c")
-        dy_d = load_own(dy, BANK + HEAD, J, "dy_d")
-        load_w4_words(nc.sync, PAGES, BLOCKS)
-        nc.sync.dma_start(out=weights[:, BANK:], in_=wgo[:, BANK:])
-        wd_3 = load_own(wd, 3 * P, 4 * P, "wd_3")
-        wd_47_and_sums = buffer(PACK * (N - 4 * P), "wd_47")
-        wd_47 = load(wd, 4 * P, N, wd_47_and_sums)
-        load_w4_scales(nc.sync, PAGES * P, N)
+        dy_1, sums_b = load(dy, *PIECES[1], "dy_1", width[0])
+        dy_2, sums_c = load(dy, *PIECES[2], "dy_2", width[1])
+        load_weights(PIECES[1][0], PIECES[2][1])
 
-        quantise_dy(weave_on_both(dy_a, "rounded_dy_a"), 0)
-        quantise_wd(weave_on_scalar(wd_0, "rounded_wd_0"), 0)
-        padded = multiply(0, -HEAD)
-        width = BANK - HEAD
-        grouped = rounded(width, "rounded_dy_b")
-        weave(nc.vector.tensor_copy, dy_b, grouped, width - LEAD, width)
-        weave(nc.scalar.copy, dy_b, grouped, 0, SCALAR_COLUMNS)
-        weave(nc.vector.tensor_copy, dy_b, grouped, SCALAR_COLUMNS, width - LEAD)
-        quantise_dy(grouped, HEAD)
-        place(0, 0, HEAD, padded, dy_b_and_sums[:, PACK * width - LEAD :])
+        grouped = rounded(width[0], "rounded_dy_0")
+        weave(nc.vector.tensor_copy, dy_0, grouped, 0, width[0] - SCALAR_COLUMNS)
+        weave(nc.scalar.copy, dy_0, grouped, width[0] - SCALAR_COLUMNS, width[0])
+        quantise(grouped, dy_codes, dy_plane, 0, E5M2)
+        grouped = rounded(P, "rounded_wd_0")
+        weave(nc.scalar.copy, wd_0, grouped, 0, P)
+        quantise(grouped, wd_codes, wd_plane, 0, E4M3)
 
-        grouped = rounded(2 * P, "rounded_wd_12")
-        for first, raw in ((0, wd_1), (P, wd_2)):
-            weave(nc.scalar.copy, raw, grouped[:, first : first + P, :], 0, P)
-        quantise_wd(grouped, P)
-        place(0, HEAD, BANK, multiply(0, 0), buffer(BANK - HEAD, "wd_2")[:])
-        pages.append(buffer(T, "rounded_wd_12"))
-        for lo in range(0, T, CLEAR):
-            nc.gpsimd.memset(pages[-1][:, lo : lo + CLEAR], 0.0)
-        place(1, 0, BANK, multiply(1, 0), buffer(BANK, "sums_1")[:])
-        grouped = rounded(J - BANK, "wd_2")
-        for first, raw in ((0, dy_c), (HEAD, dy_d)):
-            for lo in range(0, HEAD, CHUNK):
-                weave(nc.scalar.copy, raw, grouped[:, first : first + HEAD, :], lo, lo + CHUNK)
-        quantise_dy(grouped, BANK)
-        place(2, 0, BANK, multiply(2, 0), buffer(BANK, "dy_d")[:])
-
-        place(0, BANK, J, multiply(0, BANK), buffer(BANK, "sums_0")[:])
-        quantise_wd(weave_on_scalar(wd_3, "wd_2"), 3 * P)
-        place(1, BANK, J, multiply(1, BANK), buffer(BANK, "wd_3")[:])
-        place(2, BANK, J, multiply(2, BANK), buffer(BANK, "sums_2")[:])
-        quantise_wd(weave_on_scalar(wd_47, "sums_0"), 4 * P)
-
-        for b in range(PAGES, BLOCKS):
-            sums = wd_47_and_sums[:, :J] if b == PAGES else buffer(J, "sums_%d" % b)[:]
-            place(b, 0, J, multiply(b, 0) + multiply(b, BANK), sums)
+        quantise(weave_lead_first(nc.vector.tensor_copy, wd_1, "rounded_wd_1"), wd_codes, wd_plane, P, E4M3)
+        dy_3, sums_e = load(dy, *PIECES[3], "dy_3", width[2])
+        dy_4, sums_g = load(dy, *PIECES[4], "dy_4", width[3])
+        load_weights(PIECES[3][0], J)
+        load_w4_words(EARLY, BLOCKS)
+        load_w4_scales(EARLY * P, N)
+        wd_23, sums_i = load(wd, 2 * P, 4 * P, "wd_23", width[4])
+        wd_47, sums_3 = load(wd, 4 * P, N, "wd_47", J)
+        place(0, *PIECES[0], sums_a[0])
+        quantise(weave_lead_first(nc.scalar.copy, dy_1, "rounded_dy_1"), dy_codes, dy_plane, PIECES[1][0], E5M2)
+        place(1, *PIECES[0], sums_b[0])
+        later = ((dy_2, sums_c), (dy_3, sums_e), (dy_4, sums_g))
+        for i, (raw, sums) in enumerate(later, start=1):
+            quantise(weave_lead_first(nc.scalar.copy, raw, "rounded_dy_%d" % (i + 1)), dy_codes, dy_plane,
+                     PIECES[i + 1][0], E5M2)
+            if i == len(later):
+                pages.append(buffer(T, "rounded_dy_%d" % (i + 1)))
+                for lo in range(0, T, CLEAR):
+                    nc.gpsimd.memset(pages[-1][:, lo : lo + CLEAR], 0.0)
+            place(0, *PIECES[i], sums[0])
+            place(1, *PIECES[i], sums[1])
+        quantise(weave_lead_first(nc.scalar.copy, wd_23, "rounded_wd_23"), wd_codes, wd_plane, 2 * P, E4M3)
+        place(0, *PIECES[4], sums_i[0])
+        place(1, *PIECES[4], sums_i[1])
+        place(2, 0, J, buffer(J, "sums_2")[:])
+        quantise(weave_lead_first(nc.scalar.copy, wd_47, "rounded_wd_47"), wd_codes, wd_plane, 4 * P, E4M3)
+        for b in range(3, BLOCKS):
+            place(b, 0, J, sums_3[0] if b == 3 else buffer(J, "sums_%d" % b)[:])

@@ -26,10 +26,9 @@ LIST_ROWS = 16
 BLOCKS = N // P
 PAGES = 3
 EARLY = 2
-PIECES = ((0, 256), (256, 384), (384, 512), (512, 768), (768, 1024))
-SCALAR_COLUMNS = 96
+PIECES = ((0, 192), (192, 320), (320, 448), (448, 704), (704, 1024))
+WIDTHS = (128, 256, 512)
 LEAD = 32
-CLEAR = 512
 CHUNK = 128
 OVERLAP = 64
 ROUNDED_BYTES = 2 * PACK * P
@@ -45,7 +44,7 @@ def tile_list_embg_dl_none_kernel(tc, dy, w4_words, w4_scales, wd, wgo, offs, ou
 
         offsets = keep.tile([P, J // LIST_ROWS], U16, name="offsets")
         w4_codes = keep.tile([P, 2 * N], U8, name="w4_codes", align_bytes=64)
-        w4_plane = keep.tile([P, N], U8, name="w4_plane", align_bytes=64)
+        planes = [keep.tile([P, EARLY * P], U8, name="early_plane", align_bytes=64)]
         wd_codes = keep.tile([P, N], U32, name="wd_codes", align_bytes=64)
         wd_plane = keep.tile([P, N], U8, name="wd_plane", align_bytes=64)
         dy_codes = keep.tile([P, J], U32, name="dy_codes", align_bytes=64)
@@ -58,14 +57,14 @@ def tile_list_embg_dl_none_kernel(tc, dy, w4_words, w4_scales, wd, wgo, offs, ou
 
         def load(src, c0, c1, tag, sums=LEAD):
             size = PACK * (c1 - c0)
-            flat = buffer(size - LEAD + sums, tag)
-            raw = flat[:, :size].rearrange("p (t c) -> p t c", t=PACK)
+            flat = buffer(sums - LEAD + size, tag)
+            raw = flat[:, sums - LEAD :].rearrange("p (t c) -> p t c", t=PACK)
             nc.sync.dma_start(out=raw, in_=src[:, c0:c1].rearrange("(p t) c -> p t c", t=PACK))
-            return raw, (flat[:, size - LEAD :], flat[:, :sums])
+            return raw, flat[:, :sums], flat[:, size - LEAD :]
 
-        def load_w4_scales(c0, c1):
+        def load_w4_scales(plane, c0, c1):
             for q in range(QUADRANTS):
-                nc.sync.dma_start(out=w4_plane[32 * q : 32 * q + 4, c0:c1].bitcast(I32),
+                nc.sync.dma_start(out=plane[32 * q : 32 * q + 4, :].bitcast(I32),
                                   in_=w4_scales[0, 4 * q : 4 * q + 4, c0:c1].bitcast(I32))
 
         def load_w4_words(b0, b1):
@@ -84,32 +83,37 @@ def tile_list_embg_dl_none_kernel(tc, dy, w4_words, w4_scales, wd, wgo, offs, ou
             copy(out=grouped[:, lo:hi, :].rearrange("p (c i) t -> p c t i", i=LINE),
                  in_=raw[:, :, lo:hi].rearrange("p t (c i) -> p c t i", i=LINE))
 
-        def weave_lead_first(copy, raw, tag):
+        def weave_lead_first(copy, raw, tag, lead=LEAD):
             width = raw.shape[2]
             grouped = rounded(width, tag)
-            weave(copy, raw, grouped, width - LEAD, width)
-            for lo in range(0, width - LEAD, CHUNK):
-                weave(copy, raw, grouped, lo, min(lo + CHUNK, width - LEAD))
+            weave(copy, raw, grouped, 0, lead)
+            for lo in range(lead, width, CHUNK):
+                weave(copy, raw, grouped, lo, min(lo + CHUNK, width))
             return grouped
 
-        def quantise(grouped, codes, plane, c0, fmt):
-            cols = slice(c0, c0 + grouped.shape[1])
-            nc.vector.quantize_mx(out=codes[:, cols].bitcast(fmt), scales=plane[:, cols],
-                                  in_=grouped[:].rearrange("p c t -> p (c t)"))
+        def quantise(grouped, codes, plane, c0, fmt, cuts=()):
+            ends = (0, *cuts, grouped.shape[1])
+            for lo, hi in zip(ends, ends[1:]):
+                cols = slice(c0 + lo, c0 + hi)
+                nc.vector.quantize_mx(out=codes[:, cols].bitcast(fmt), scales=plane[:, cols],
+                                      in_=grouped[:, lo:hi, :].rearrange("p c t -> p (c t)"))
 
-        def place(b, c0, c1, sums):
+        def place(b, c0, c1, sums, cuts=()):
             rows = slice(b * P, (b + 1) * P)
-            for lo in range(c0, c1, BANK):
-                hi = min(lo + BANK, c1)
+            w4_scale = planes[0][:, rows] if b < EARLY else planes[1][:, (b - EARLY) * P : (b - EARLY + 1) * P]
+            ends = (c0, *cuts, c1)
+            for lo, hi in zip(ends, ends[1:]):
+                width = min(w for w in WIDTHS if w >= hi - lo)
+                cols = slice(hi - width, hi)
                 acc = psum.tile([P, BANK], F32, name="acc")
-                moving = dy_codes[:, lo:hi].bitcast(E5M2)
-                nc.tensor.matmul_mx(out=acc[:, : hi - lo], lhsT=w4_codes[:, 2 * b * P : 2 * (b + 1) * P].bitcast(E2M1),
-                                    lhsT_scale=w4_plane[:, rows], rhs=moving, rhs_scale=dy_plane[:, lo:hi],
+                moving = dy_codes[:, cols].bitcast(E5M2)
+                nc.tensor.matmul_mx(out=acc[:, :width], lhsT=w4_codes[:, 2 * b * P : 2 * (b + 1) * P].bitcast(E2M1),
+                                    lhsT_scale=w4_scale, rhs=moving, rhs_scale=dy_plane[:, cols],
                                     start=True, stop=False)
-                nc.tensor.matmul_mx(out=acc[:, : hi - lo], lhsT=wd_codes[:, rows].bitcast(E4M3),
-                                    lhsT_scale=wd_plane[:, rows], rhs=moving, rhs_scale=dy_plane[:, lo:hi],
+                nc.tensor.matmul_mx(out=acc[:, :width], lhsT=wd_codes[:, rows].bitcast(E4M3),
+                                    lhsT_scale=wd_plane[:, rows], rhs=moving, rhs_scale=dy_plane[:, cols],
                                     start=False, stop=True)
-                nc.scalar.copy(out=sums[:, lo - c0 : hi - c0], in_=acc[:, : hi - lo])
+                nc.scalar.copy(out=sums[:, lo - c0 : hi - c0], in_=acc[:, width - (hi - lo) : width])
             window = pages[b % PAGES][:].indirect(offsets[:, c0 // LIST_ROWS : c1 // LIST_ROWS])
             nc.vector.tensor_tensor(window, sums, weights[:, c0:c1], MULT)
             if c1 == J:
@@ -120,55 +124,56 @@ def tile_list_embg_dl_none_kernel(tc, dy, w4_words, w4_scales, wd, wgo, offs, ou
             nc.vector.memset(view[:, :cut], value)
             nc.vector.memset(view[:, cut:], value)
 
-        clear_in_odd_halves(w4_plane[:].bitcast(U32), 0)
+        clear_in_odd_halves(planes[0][:].bitcast(U32), 0)
         clear_in_odd_halves(pages[0][:], 0.0)
         nc.gpsimd.memset(pages[1][:], 0.0)
 
         width = [c1 - c0 for c0, c1 in PIECES]
-        dy_0, spare = load(dy, *PIECES[0], "dy_0")
-        wd_0, spare = load(wd, 0, P, "wd_0")
+        dy_0 = load(dy, *PIECES[0], "dy_0")[0]
+        wd_0 = load(wd, 0, P, "wd_0")[0]
         load_w4_words(0, EARLY)
-        load_w4_scales(0, EARLY * P)
-        wd_1, sums_a = load(wd, P, 2 * P, "wd_1", width[0])
+        load_w4_scales(planes[0], 0, EARLY * P)
+        wd_1 = load(wd, P, 2 * P, "wd_1", width[0])
         load_weights(*PIECES[0])
         nc.sync.dma_start(offsets[:], offs)
-        dy_1, sums_b = load(dy, *PIECES[1], "dy_1", width[0])
-        dy_2, sums_c = load(dy, *PIECES[2], "dy_2", width[1])
+        dy_1 = load(dy, *PIECES[1], "dy_1", width[0])
+        dy_2 = load(dy, *PIECES[2], "dy_2", width[1])
         load_weights(PIECES[1][0], PIECES[2][1])
+        dy_3 = load(dy, *PIECES[3], "dy_3", width[2])
+        dy_4 = load(dy, *PIECES[4], "dy_4", width[3])
+        load_weights(PIECES[3][0], J)
+        load_w4_words(EARLY, BLOCKS)
 
         grouped = rounded(width[0], "rounded_dy_0")
-        weave(nc.vector.tensor_copy, dy_0, grouped, 0, width[0] - SCALAR_COLUMNS)
-        weave(nc.scalar.copy, dy_0, grouped, width[0] - SCALAR_COLUMNS, width[0])
-        quantise(grouped, dy_codes, dy_plane, 0, E5M2)
+        weave(nc.scalar.copy, dy_0, grouped, 0, 64)
+        weave(nc.vector.tensor_copy, dy_0, grouped, 64, width[0])
+        planes.append(keep.tile([P, N - EARLY * P], U8, name="late_plane", tag="dy_0", align_bytes=64))
+        nc.vector.memset(planes[1][:].bitcast(U32), 0)
+        load_w4_scales(planes[1], EARLY * P, N)
+        wd_23 = load(wd, 2 * P, 4 * P, "wd_23", width[4])
+        wd_47 = load(wd, 4 * P, N, "wd_47", J)
+        quantise(grouped, dy_codes, dy_plane, 0, E5M2, (64,))
         grouped = rounded(P, "rounded_wd_0")
         weave(nc.scalar.copy, wd_0, grouped, 0, P)
         quantise(grouped, wd_codes, wd_plane, 0, E4M3)
 
-        quantise(weave_lead_first(nc.vector.tensor_copy, wd_1, "rounded_wd_1"), wd_codes, wd_plane, P, E4M3)
-        dy_3, sums_e = load(dy, *PIECES[3], "dy_3", width[2])
-        dy_4, sums_g = load(dy, *PIECES[4], "dy_4", width[3])
-        load_weights(PIECES[3][0], J)
-        load_w4_words(EARLY, BLOCKS)
-        load_w4_scales(EARLY * P, N)
-        wd_23, sums_i = load(wd, 2 * P, 4 * P, "wd_23", width[4])
-        wd_47, sums_3 = load(wd, 4 * P, N, "wd_47", J)
-        place(0, *PIECES[0], sums_a[0])
-        quantise(weave_lead_first(nc.scalar.copy, dy_1, "rounded_dy_1"), dy_codes, dy_plane, PIECES[1][0], E5M2)
-        place(1, *PIECES[0], sums_b[0])
-        later = ((dy_2, sums_c), (dy_3, sums_e), (dy_4, sums_g))
-        for i, (raw, sums) in enumerate(later, start=1):
+        quantise(weave_lead_first(nc.vector.tensor_copy, wd_1[0], "rounded_wd_1", 2 * LEAD), wd_codes, wd_plane, P, E4M3)
+        place(0, *PIECES[0], wd_1[1], (P,))
+        quantise(weave_lead_first(nc.scalar.copy, dy_1[0], "rounded_dy_1"), dy_codes, dy_plane, PIECES[1][0], E5M2)
+        place(1, *PIECES[0], dy_1[1], (P,))
+        later = (dy_2, dy_3, dy_4)
+        for i, (raw, first, second) in enumerate(later, start=1):
             quantise(weave_lead_first(nc.scalar.copy, raw, "rounded_dy_%d" % (i + 1)), dy_codes, dy_plane,
-                     PIECES[i + 1][0], E5M2)
+                     PIECES[i + 1][0], E5M2, (256,) if raw.shape[2] > 256 else ())
             if i == len(later):
                 pages.append(buffer(T, "rounded_dy_%d" % (i + 1)))
-                for lo in range(0, T, CLEAR):
-                    nc.gpsimd.memset(pages[-1][:, lo : lo + CLEAR], 0.0)
-            place(0, *PIECES[i], sums[0])
-            place(1, *PIECES[i], sums[1])
-        quantise(weave_lead_first(nc.scalar.copy, wd_23, "rounded_wd_23"), wd_codes, wd_plane, 2 * P, E4M3)
-        place(0, *PIECES[4], sums_i[0])
-        place(1, *PIECES[4], sums_i[1])
-        place(2, 0, J, buffer(J, "sums_2")[:])
-        quantise(weave_lead_first(nc.scalar.copy, wd_47, "rounded_wd_47"), wd_codes, wd_plane, 4 * P, E4M3)
+                nc.gpsimd.memset(pages[-1][:], 0.0)
+            place(0, *PIECES[i], first)
+            place(1, *PIECES[i], second)
+        quantise(weave_lead_first(nc.scalar.copy, wd_23[0], "rounded_wd_23"), wd_codes, wd_plane, 2 * P, E4M3)
+        place(0, *PIECES[4], wd_23[1])
+        place(1, *PIECES[4], wd_23[2])
+        place(2, 0, J, buffer(J, "sums_2")[:], (BANK,))
+        quantise(weave_lead_first(nc.scalar.copy, wd_47[0], "rounded_wd_47"), wd_codes, wd_plane, 4 * P, E4M3)
         for b in range(3, BLOCKS):
-            place(b, 0, J, sums_3[0] if b == 3 else buffer(J, "sums_%d" % b)[:])
+            place(b, 0, J, wd_47[1] if b == 3 else buffer(J, "sums_%d" % b)[:], (BANK,))

@@ -30,6 +30,7 @@ PIECES = ((0, 192), (192, 320), (320, 448), (448, 704), (704, 1024))
 WIDTHS = (128, 256, 512)
 LEAD = 32
 CHUNK = 128
+SHIFTED = 384
 OVERLAP = 64
 ROUNDED_BYTES = 2 * PACK * P
 RING = {"rounded_dy_1": 0, "rounded_wd_0": ROUNDED_BYTES - OVERLAP, "rounded_wd_1": ROUNDED_BYTES - OVERLAP}
@@ -126,7 +127,8 @@ def tile_list_embg_dl_none_kernel(tc, dy, w4_words, w4_scales, wd, wgo, offs, ou
 
         clear_in_odd_halves(planes[0][:].bitcast(U32), 0)
         clear_in_odd_halves(pages[0][:], 0.0)
-        nc.gpsimd.memset(pages[1][:], 0.0)
+        clear_in_odd_halves(pages[1][:, :SHIFTED], 0.0)
+        nc.gpsimd.memset(pages[1][:, SHIFTED:], 0.0)
 
         width = [c1 - c0 for c0, c1 in PIECES]
         dy_0 = load(dy, *PIECES[0], "dy_0")[0]

@@ -26,21 +26,20 @@ LIST_ROWS = 16
 BLOCKS = N // P
 PAGES = 3
 EARLY = 2
-PIECES = ((0, 192), (192, 320), (320, 448), (448, 704), (704, 1024))
+CUTS = (0, 128, 256, 384, 576, 832, 1024)
+PIECES = tuple(zip(CUTS, CUTS[1:]))
 WIDTHS = (128, 256, 512)
+QUANT_WIDTHS = (512, 256, 128, 64)
 LEAD = 32
 CHUNK = 128
-SHIFTED = 384
-OVERLAP = 64
-ROUNDED_BYTES = 2 * PACK * P
-RING = {"rounded_dy_1": 0, "rounded_wd_0": ROUNDED_BYTES - OVERLAP, "rounded_wd_1": ROUNDED_BYTES - OVERLAP}
+SCALAR_TOKENS = 32
+VECTOR_CLEARS = 384
 
 
 def tile_list_embg_dl_none_kernel(tc, dy, w4_words, w4_scales, wd, wgo, offs, out):
     nc = tc.nc
     with ExitStack() as ctx:
         keep = ctx.enter_context(tc.tile_pool(name="keep", bufs=1))
-        ring = ctx.enter_context(tc.tile_pool(name="ring", bufs=1))
         psum = ctx.enter_context(tc.psum_pool(name="psum", bufs=PSUM_BANKS))
 
         offsets = keep.tile([P, J // LIST_ROWS], U16, name="offsets")
@@ -76,28 +75,28 @@ def tile_list_embg_dl_none_kernel(tc, dy, w4_words, w4_scales, wd, wgo, offs, ou
             nc.sync.dma_start(out=weights[:, c0:c1], in_=wgo[:, c0:c1])
 
         def rounded(columns, tag):
-            if tag in RING:
-                return ring.tile([P, columns, PACK], BF16, name=tag, align_bytes=64, offset=RING[tag])
             return keep.tile([P, columns, PACK], BF16, name="rounded", tag=tag, align_bytes=64)
 
-        def weave(copy, raw, grouped, lo, hi):
-            copy(out=grouped[:, lo:hi, :].rearrange("p (c i) t -> p c t i", i=LINE),
+        def weave(copy, raw, grouped, lo, hi, shift=0):
+            copy(out=grouped[:, lo - shift : hi - shift, :].rearrange("p (c i) t -> p c t i", i=LINE),
                  in_=raw[:, :, lo:hi].rearrange("p t (c i) -> p c t i", i=LINE))
 
-        def weave_lead_first(copy, raw, tag, lead=LEAD):
+        def weave_lead_first(raw, tag):
             width = raw.shape[2]
             grouped = rounded(width, tag)
-            weave(copy, raw, grouped, 0, lead)
-            for lo in range(lead, width, CHUNK):
-                weave(copy, raw, grouped, lo, min(lo + CHUNK, width))
+            weave(nc.scalar.copy, raw, grouped, 0, LEAD)
+            for lo in range(LEAD, width, CHUNK):
+                weave(nc.scalar.copy, raw, grouped, lo, min(lo + CHUNK, width))
             return grouped
 
-        def quantise(grouped, codes, plane, c0, fmt, cuts=()):
-            ends = (0, *cuts, grouped.shape[1])
-            for lo, hi in zip(ends, ends[1:]):
+        def quantise(grouped, codes, plane, c0, fmt):
+            lo = 0
+            while lo < grouped.shape[1]:
+                hi = lo + max(w for w in QUANT_WIDTHS if w <= grouped.shape[1] - lo)
                 cols = slice(c0 + lo, c0 + hi)
                 nc.vector.quantize_mx(out=codes[:, cols].bitcast(fmt), scales=plane[:, cols],
                                       in_=grouped[:, lo:hi, :].rearrange("p c t -> p (c t)"))
+                lo = hi
 
         def place(b, c0, c1, sums, cuts=()):
             rows = slice(b * P, (b + 1) * P)
@@ -108,11 +107,11 @@ def tile_list_embg_dl_none_kernel(tc, dy, w4_words, w4_scales, wd, wgo, offs, ou
                 cols = slice(hi - width, hi)
                 acc = psum.tile([P, BANK], F32, name="acc")
                 moving = dy_codes[:, cols].bitcast(E5M2)
-                nc.tensor.matmul_mx(out=acc[:, :width], lhsT=w4_codes[:, 2 * b * P : 2 * (b + 1) * P].bitcast(E2M1),
-                                    lhsT_scale=w4_scale, rhs=moving, rhs_scale=dy_plane[:, cols],
-                                    start=True, stop=False)
                 nc.tensor.matmul_mx(out=acc[:, :width], lhsT=wd_codes[:, rows].bitcast(E4M3),
                                     lhsT_scale=wd_plane[:, rows], rhs=moving, rhs_scale=dy_plane[:, cols],
+                                    start=True, stop=False)
+                nc.tensor.matmul_mx(out=acc[:, :width], lhsT=w4_codes[:, 2 * b * P : 2 * (b + 1) * P].bitcast(E2M1),
+                                    lhsT_scale=w4_scale, rhs=moving, rhs_scale=dy_plane[:, cols],
                                     start=False, stop=True)
                 nc.scalar.copy(out=sums[:, lo - c0 : hi - c0], in_=acc[:, width - (hi - lo) : width])
             window = pages[b % PAGES][:].indirect(offsets[:, c0 // LIST_ROWS : c1 // LIST_ROWS])
@@ -127,55 +126,55 @@ def tile_list_embg_dl_none_kernel(tc, dy, w4_words, w4_scales, wd, wgo, offs, ou
 
         clear_in_odd_halves(planes[0][:].bitcast(U32), 0)
         clear_in_odd_halves(pages[0][:], 0.0)
-        clear_in_odd_halves(pages[1][:, :SHIFTED], 0.0)
-        nc.gpsimd.memset(pages[1][:, SHIFTED:], 0.0)
+        clear_in_odd_halves(pages[1][:, :VECTOR_CLEARS], 0.0)
+        nc.gpsimd.memset(pages[1][:, VECTOR_CLEARS:], 0.0)
 
         width = [c1 - c0 for c0, c1 in PIECES]
-        dy_0 = load(dy, *PIECES[0], "dy_0")[0]
-        wd_0 = load(wd, 0, P, "wd_0")[0]
+        wd_01 = load(wd, 0, EARLY * P, "wd_01")[0]
+        pieces = [load(dy, *PIECES[0], "dy_0")]
         load_w4_words(0, EARLY)
         load_w4_scales(planes[0], 0, EARLY * P)
-        wd_1 = load(wd, P, 2 * P, "wd_1", width[0])
         load_weights(*PIECES[0])
+        pieces.append(load(dy, *PIECES[1], "dy_1", width[0]))
         nc.sync.dma_start(offsets[:], offs)
-        dy_1 = load(dy, *PIECES[1], "dy_1", width[0])
-        dy_2 = load(dy, *PIECES[2], "dy_2", width[1])
-        load_weights(PIECES[1][0], PIECES[2][1])
-        dy_3 = load(dy, *PIECES[3], "dy_3", width[2])
-        dy_4 = load(dy, *PIECES[4], "dy_4", width[3])
-        load_weights(PIECES[3][0], J)
+        pieces.append(load(dy, *PIECES[2], "dy_2", width[1]))
+        load_weights(CUTS[1], CUTS[3])
+        pieces.append(load(dy, *PIECES[3], "dy_3", width[2]))
+        pieces.append(load(dy, *PIECES[4], "dy_4", width[3]))
+        load_weights(CUTS[3], J)
+        pieces.append(load(dy, *PIECES[5], "dy_5", width[4]))
         load_w4_words(EARLY, BLOCKS)
 
+        wd_rounded = [rounded(P, "rounded_wd_%d" % b) for b in range(EARLY)]
+        weave(nc.vector.tensor_copy, wd_01, wd_rounded[0], 0, P)
+        weave(nc.scalar.copy, wd_01, wd_rounded[1], P, 2 * P, P)
+        quantise(wd_rounded[0], wd_codes, wd_plane, 0, E4M3)
         grouped = rounded(width[0], "rounded_dy_0")
-        weave(nc.scalar.copy, dy_0, grouped, 0, 64)
-        weave(nc.vector.tensor_copy, dy_0, grouped, 64, width[0])
-        planes.append(keep.tile([P, N - EARLY * P], U8, name="late_plane", tag="dy_0", align_bytes=64))
+        weave(nc.vector.tensor_copy, pieces[0][0], grouped, SCALAR_TOKENS, width[0])
+        weave(nc.scalar.copy, pieces[0][0], grouped, 0, SCALAR_TOKENS)
+        quantise(grouped, dy_codes, dy_plane, 0, E5M2)
+        quantise(wd_rounded[1], wd_codes, wd_plane, P, E4M3)
+        planes.append(keep.tile([P, N - EARLY * P], U8, name="late_plane", tag="rounded_dy_0", align_bytes=64))
         nc.vector.memset(planes[1][:].bitcast(U32), 0)
         load_w4_scales(planes[1], EARLY * P, N)
-        wd_23 = load(wd, 2 * P, 4 * P, "wd_23", width[4])
+        wd_23 = load(wd, 2 * P, 4 * P, "wd_23", width[-1])
         wd_47 = load(wd, 4 * P, N, "wd_47", J)
-        quantise(grouped, dy_codes, dy_plane, 0, E5M2, (64,))
-        grouped = rounded(P, "rounded_wd_0")
-        weave(nc.scalar.copy, wd_0, grouped, 0, P)
-        quantise(grouped, wd_codes, wd_plane, 0, E4M3)
 
-        quantise(weave_lead_first(nc.vector.tensor_copy, wd_1[0], "rounded_wd_1", 2 * LEAD), wd_codes, wd_plane, P, E4M3)
-        place(0, *PIECES[0], wd_1[1], (P,))
-        quantise(weave_lead_first(nc.scalar.copy, dy_1[0], "rounded_dy_1"), dy_codes, dy_plane, PIECES[1][0], E5M2)
-        place(1, *PIECES[0], dy_1[1], (P,))
-        later = (dy_2, dy_3, dy_4)
-        for i, (raw, first, second) in enumerate(later, start=1):
-            quantise(weave_lead_first(nc.scalar.copy, raw, "rounded_dy_%d" % (i + 1)), dy_codes, dy_plane,
-                     PIECES[i + 1][0], E5M2, (256,) if raw.shape[2] > 256 else ())
-            if i == len(later):
+        place(0, *PIECES[0], buffer(width[0], "sums_0")[:])
+        quantise(weave_lead_first(pieces[1][0], "rounded_wd_1"), dy_codes, dy_plane, CUTS[1], E5M2)
+        place(1, *PIECES[0], pieces[1][2])
+        for i in range(1, len(PIECES) - 1):
+            raw, first, second = pieces[i + 1]
+            quantise(weave_lead_first(raw, "rounded_dy_%d" % (i + 1)), dy_codes, dy_plane, CUTS[i + 1], E5M2)
+            if i == len(PIECES) - 2:
                 pages.append(buffer(T, "rounded_dy_%d" % (i + 1)))
                 nc.gpsimd.memset(pages[-1][:], 0.0)
             place(0, *PIECES[i], first)
             place(1, *PIECES[i], second)
-        quantise(weave_lead_first(nc.scalar.copy, wd_23[0], "rounded_wd_23"), wd_codes, wd_plane, 2 * P, E4M3)
-        place(0, *PIECES[4], wd_23[1])
-        place(1, *PIECES[4], wd_23[2])
+        quantise(weave_lead_first(wd_23[0], "rounded_wd_23"), wd_codes, wd_plane, 2 * P, E4M3)
+        place(0, *PIECES[-1], wd_23[1])
+        place(1, *PIECES[-1], wd_23[2])
         place(2, 0, J, buffer(J, "sums_2")[:], (BANK,))
-        quantise(weave_lead_first(nc.scalar.copy, wd_47[0], "rounded_wd_47"), wd_codes, wd_plane, 4 * P, E4M3)
+        quantise(weave_lead_first(wd_47[0], "rounded_wd_47"), wd_codes, wd_plane, 4 * P, E4M3)
         for b in range(3, BLOCKS):
             place(b, 0, J, wd_47[1] if b == 3 else buffer(J, "sums_%d" % b)[:], (BANK,))

@@ -26,14 +26,14 @@ LIST_ROWS = 16
 BLOCKS = N // P
 PAGES = 3
 EARLY = 2
-CUTS = (0, 128, 256, 384, 576, 832, 1024)
+CUTS = (0, 128, 256, 384, 640, 1024)
 PIECES = tuple(zip(CUTS, CUTS[1:]))
 WIDTHS = (128, 256, 512)
-QUANT_WIDTHS = (512, 256, 128, 64)
+QUANT_WIDTHS = (512, 256, 128)
 LEAD = 32
 CHUNK = 128
-SCALAR_TOKENS = 32
-VECTOR_CLEARS = 384
+SCALAR_SHARE = 48
+VECTOR_CLEARS = 128
 
 
 def tile_list_embg_dl_none_kernel(tc, dy, w4_words, w4_scales, wd, wgo, offs, out):
@@ -44,7 +44,8 @@ def tile_list_embg_dl_none_kernel(tc, dy, w4_words, w4_scales, wd, wgo, offs, ou
 
         offsets = keep.tile([P, J // LIST_ROWS], U16, name="offsets")
         w4_codes = keep.tile([P, 2 * N], U8, name="w4_codes", align_bytes=64)
-        planes = [keep.tile([P, EARLY * P], U8, name="early_plane", align_bytes=64)]
+        planes = [keep.tile([P, EARLY * P], U8, name="early_plane", align_bytes=64),
+                  keep.tile([P, N - EARLY * P], U8, name="late_plane", align_bytes=64)]
         wd_codes = keep.tile([P, N], U32, name="wd_codes", align_bytes=64)
         wd_plane = keep.tile([P, N], U8, name="wd_plane", align_bytes=64)
         dy_codes = keep.tile([P, J], U32, name="dy_codes", align_bytes=64)
@@ -67,6 +68,11 @@ def tile_list_embg_dl_none_kernel(tc, dy, w4_words, w4_scales, wd, wgo, offs, ou
                 nc.sync.dma_start(out=plane[32 * q : 32 * q + 4, :].bitcast(I32),
                                   in_=w4_scales[0, 4 * q : 4 * q + 4, c0:c1].bitcast(I32))
 
+        def load_early_scales(quadrants):
+            for q in quadrants:
+                rows = w4_scales[0, 4 * q : 4 * q + 4, : EARLY * P].bitcast(I32)
+                nc.sync.dma_start(out=planes[0][32 * q : 32 * q + 32, :].bitcast(I32), in_=rows.partition_broadcast(8))
+
         def load_w4_words(b0, b1):
             cols = slice(b0 * P // 2, b1 * P // 2)
             nc.sync.dma_start(out=w4_codes[:].bitcast(I32)[:, cols], in_=w4_words[0].bitcast(I32)[:, cols])
@@ -81,12 +87,18 @@ def tile_list_embg_dl_none_kernel(tc, dy, w4_words, w4_scales, wd, wgo, offs, ou
             copy(out=grouped[:, lo - shift : hi - shift, :].rearrange("p (c i) t -> p c t i", i=LINE),
                  in_=raw[:, :, lo:hi].rearrange("p t (c i) -> p c t i", i=LINE))
 
-        def weave_lead_first(raw, tag):
+        def weave_lead_first(raw, tag, chunk=CHUNK):
             width = raw.shape[2]
             grouped = rounded(width, tag)
             weave(nc.scalar.copy, raw, grouped, 0, LEAD)
-            for lo in range(LEAD, width, CHUNK):
-                weave(nc.scalar.copy, raw, grouped, lo, min(lo + CHUNK, width))
+            for lo in range(LEAD, width, chunk):
+                weave(nc.scalar.copy, raw, grouped, lo, min(lo + chunk, width))
+            return grouped
+
+        def weave_shared(raw, tag, c0, scalar_share):
+            grouped = rounded(P, tag)
+            weave(nc.scalar.copy, raw, grouped, c0, c0 + scalar_share, c0)
+            weave(nc.vector.tensor_copy, raw, grouped, c0 + scalar_share, c0 + P, c0)
             return grouped
 
         def quantise(grouped, codes, plane, c0, fmt):
@@ -107,11 +119,11 @@ def tile_list_embg_dl_none_kernel(tc, dy, w4_words, w4_scales, wd, wgo, offs, ou
                 cols = slice(hi - width, hi)
                 acc = psum.tile([P, BANK], F32, name="acc")
                 moving = dy_codes[:, cols].bitcast(E5M2)
-                nc.tensor.matmul_mx(out=acc[:, :width], lhsT=wd_codes[:, rows].bitcast(E4M3),
-                                    lhsT_scale=wd_plane[:, rows], rhs=moving, rhs_scale=dy_plane[:, cols],
-                                    start=True, stop=False)
                 nc.tensor.matmul_mx(out=acc[:, :width], lhsT=w4_codes[:, 2 * b * P : 2 * (b + 1) * P].bitcast(E2M1),
                                     lhsT_scale=w4_scale, rhs=moving, rhs_scale=dy_plane[:, cols],
+                                    start=True, stop=False)
+                nc.tensor.matmul_mx(out=acc[:, :width], lhsT=wd_codes[:, rows].bitcast(E4M3),
+                                    lhsT_scale=wd_plane[:, rows], rhs=moving, rhs_scale=dy_plane[:, cols],
                                     start=False, stop=True)
                 nc.scalar.copy(out=sums[:, lo - c0 : hi - c0], in_=acc[:, width - (hi - lo) : width])
             window = pages[b % PAGES][:].indirect(offsets[:, c0 // LIST_ROWS : c1 // LIST_ROWS])
@@ -124,48 +136,41 @@ def tile_list_embg_dl_none_kernel(tc, dy, w4_words, w4_scales, wd, wgo, offs, ou
             nc.vector.memset(view[:, :cut], value)
             nc.vector.memset(view[:, cut:], value)
 
-        clear_in_odd_halves(planes[0][:].bitcast(U32), 0)
         clear_in_odd_halves(pages[0][:], 0.0)
+        clear_in_odd_halves(planes[1][:].bitcast(U32), 0)
         clear_in_odd_halves(pages[1][:, :VECTOR_CLEARS], 0.0)
         nc.gpsimd.memset(pages[1][:, VECTOR_CLEARS:], 0.0)
 
         width = [c1 - c0 for c0, c1 in PIECES]
-        wd_01 = load(wd, 0, EARLY * P, "wd_01")[0]
         pieces = [load(dy, *PIECES[0], "dy_0")]
+        load_early_scales((0, 1))
+        wd_01 = load(wd, 0, EARLY * P, "wd_01")[0]
+        load_early_scales((2, 3))
         load_w4_words(0, EARLY)
-        load_w4_scales(planes[0], 0, EARLY * P)
-        load_weights(*PIECES[0])
-        pieces.append(load(dy, *PIECES[1], "dy_1", width[0]))
+        pieces.append(load(dy, *PIECES[1], "dy_1"))
+        load_weights(0, CUTS[3])
         nc.sync.dma_start(offsets[:], offs)
-        pieces.append(load(dy, *PIECES[2], "dy_2", width[1]))
-        load_weights(CUTS[1], CUTS[3])
-        pieces.append(load(dy, *PIECES[3], "dy_3", width[2]))
-        pieces.append(load(dy, *PIECES[4], "dy_4", width[3]))
+        for i in range(2, len(PIECES)):
+            pieces.append(load(dy, *PIECES[i], "dy_%d" % i, width[i - 1]))
         load_weights(CUTS[3], J)
-        pieces.append(load(dy, *PIECES[5], "dy_5", width[4]))
         load_w4_words(EARLY, BLOCKS)
 
-        wd_rounded = [rounded(P, "rounded_wd_%d" % b) for b in range(EARLY)]
-        weave(nc.vector.tensor_copy, wd_01, wd_rounded[0], 0, P)
-        weave(nc.scalar.copy, wd_01, wd_rounded[1], P, 2 * P, P)
-        quantise(wd_rounded[0], wd_codes, wd_plane, 0, E4M3)
-        grouped = rounded(width[0], "rounded_dy_0")
-        weave(nc.vector.tensor_copy, pieces[0][0], grouped, SCALAR_TOKENS, width[0])
-        weave(nc.scalar.copy, pieces[0][0], grouped, 0, SCALAR_TOKENS)
-        quantise(grouped, dy_codes, dy_plane, 0, E5M2)
-        quantise(wd_rounded[1], wd_codes, wd_plane, P, E4M3)
-        planes.append(keep.tile([P, N - EARLY * P], U8, name="late_plane", tag="rounded_dy_0", align_bytes=64))
-        nc.vector.memset(planes[1][:].bitcast(U32), 0)
+        quantise(weave_shared(pieces[0][0], "rounded_dy_0", 0, SCALAR_SHARE), dy_codes, dy_plane, 0, E5M2)
+        wd_rounded = [weave_shared(wd_01, "rounded_wd_0", 0, SCALAR_SHARE), weave_shared(wd_01, "rounded_wd_1", P, P // 2)]
+        for b in range(EARLY):
+            quantise(wd_rounded[b], wd_codes, wd_plane, b * P, E4M3)
+        grouped = rounded(width[1], "rounded_dy_1")
+        weave(nc.vector.tensor_copy, pieces[1][0], grouped, 0, width[1])
+        quantise(grouped, dy_codes, dy_plane, CUTS[1], E5M2)
         load_w4_scales(planes[1], EARLY * P, N)
         wd_23 = load(wd, 2 * P, 4 * P, "wd_23", width[-1])
         wd_47 = load(wd, 4 * P, N, "wd_47", J)
 
-        place(0, *PIECES[0], buffer(width[0], "sums_0")[:])
-        quantise(weave_lead_first(pieces[1][0], "rounded_wd_1"), dy_codes, dy_plane, CUTS[1], E5M2)
-        place(1, *PIECES[0], pieces[1][2])
+        for b in range(EARLY):
+            place(b, *PIECES[0], buffer(width[0], "sums_%d" % b)[:])
         for i in range(1, len(PIECES) - 1):
             raw, first, second = pieces[i + 1]
-            quantise(weave_lead_first(raw, "rounded_dy_%d" % (i + 1)), dy_codes, dy_plane, CUTS[i + 1], E5M2)
+            quantise(weave_lead_first(raw, "rounded_dy_%d" % (i + 1), J), dy_codes, dy_plane, CUTS[i + 1], E5M2)
             if i == len(PIECES) - 2:
                 pages.append(buffer(T, "rounded_dy_%d" % (i + 1)))
                 nc.gpsimd.memset(pages[-1][:], 0.0)

@@ -63,15 +63,10 @@ def tile_list_embg_dl_none_kernel(tc, dy, w4_words, w4_scales, wd, wgo, offs, ou
             nc.sync.dma_start(out=raw, in_=src[:, c0:c1].rearrange("(p t) c -> p t c", t=PACK))
             return raw, flat[:, :sums], flat[:, size - LEAD :]
 
-        def load_w4_scales(plane, c0, c1):
-            for q in range(QUADRANTS):
+        def load_w4_scales(plane, c0, c1, quadrants=range(QUADRANTS)):
+            for q in quadrants:
                 nc.sync.dma_start(out=plane[32 * q : 32 * q + 4, :].bitcast(I32),
                                   in_=w4_scales[0, 4 * q : 4 * q + 4, c0:c1].bitcast(I32))
-
-        def load_early_scales(quadrants):
-            for q in quadrants:
-                rows = w4_scales[0, 4 * q : 4 * q + 4, : EARLY * P].bitcast(I32)
-                nc.sync.dma_start(out=planes[0][32 * q : 32 * q + 32, :].bitcast(I32), in_=rows.partition_broadcast(8))
 
         def load_w4_words(b0, b1):
             cols = slice(b0 * P // 2, b1 * P // 2)
@@ -136,6 +131,7 @@ def tile_list_embg_dl_none_kernel(tc, dy, w4_words, w4_scales, wd, wgo, offs, ou
             nc.vector.memset(view[:, :cut], value)
             nc.vector.memset(view[:, cut:], value)
 
+        nc.vector.memset(planes[0][:].bitcast(U32), 0)
         clear_in_odd_halves(pages[0][:], 0.0)
         clear_in_odd_halves(planes[1][:].bitcast(U32), 0)
         clear_in_odd_halves(pages[1][:, :VECTOR_CLEARS], 0.0)
@@ -143,9 +139,9 @@ def tile_list_embg_dl_none_kernel(tc, dy, w4_words, w4_scales, wd, wgo, offs, ou
 
         width = [c1 - c0 for c0, c1 in PIECES]
         pieces = [load(dy, *PIECES[0], "dy_0")]
-        load_early_scales((0, 1))
+        load_w4_scales(planes[0], 0, EARLY * P, (0, 1))
         wd_01 = load(wd, 0, EARLY * P, "wd_01")[0]
-        load_early_scales((2, 3))
+        load_w4_scales(planes[0], 0, EARLY * P, (2, 3))
         load_w4_words(0, EARLY)
         pieces.append(load(dy, *PIECES[1], "dy_1"))
         load_weights(0, CUTS[3])

@@ -131,7 +131,7 @@ def tile_list_embg_dl_none_kernel(tc, dy, w4_words, w4_scales, wd, wgo, offs, ou
             nc.vector.memset(view[:, :cut], value)
             nc.vector.memset(view[:, cut:], value)
 
-        nc.vector.memset(planes[0][:].bitcast(U32), 0)
+        clear_in_odd_halves(planes[0][:].bitcast(U32), 0)
         clear_in_odd_halves(pages[0][:], 0.0)
         clear_in_odd_halves(planes[1][:].bitcast(U32), 0)
         clear_in_odd_halves(pages[1][:, :VECTOR_CLEARS], 0.0)

@@ -139,9 +139,9 @@ def tile_list_embg_dl_none_kernel(tc, dy, w4_words, w4_scales, wd, wgo, offs, ou
 
         width = [c1 - c0 for c0, c1 in PIECES]
         pieces = [load(dy, *PIECES[0], "dy_0")]
-        load_w4_scales(planes[0], 0, EARLY * P, (0, 1))
+        load_w4_scales(planes[0], 0, EARLY * P, (0,))
         wd_01 = load(wd, 0, EARLY * P, "wd_01")[0]
-        load_w4_scales(planes[0], 0, EARLY * P, (2, 3))
+        load_w4_scales(planes[0], 0, EARLY * P, (1, 2, 3))
         load_w4_words(0, EARLY)
         pieces.append(load(dy, *PIECES[1], "dy_1"))
         load_weights(0, CUTS[3])

from contextlib import ExitStack

import concourse.mybir as mybir

K, N, T, J = 512, 1024, 2048, 1024
FLOPS = 2 * 2 * K * N * J

F32 = mybir.dt.float32
BF16 = mybir.dt.bfloat16
I32 = mybir.dt.int32
U32 = mybir.dt.uint32
U16 = mybir.dt.uint16
U8 = mybir.dt.uint8
E4M3 = mybir.dt.float8_e4m3fn_x4
E5M2 = mybir.dt.float8_e5m2_x4
E2M1 = mybir.dt.float4_e2m1fn_x4
MULT = mybir.AluOpType.mult

P = 128
PACK = 4
LINE = 4
BANK = 512
PSUM_BANKS = 8
QUADRANTS = 4
LIST_ROWS = 16
BLOCKS = N // P
PAGES = 3
EARLY = 2
CUTS = (0, 128, 256, 384, 640, 1024)
PIECES = tuple(zip(CUTS, CUTS[1:]))
WIDTHS = (128, 256, 512)
QUANT_WIDTHS = (512, 256, 128)
LEAD = 32
CHUNK = 128
SCALAR_SHARE = 48
VECTOR_CLEARS = 128


def tile_list_embg_dl_none_kernel(tc, dy, w4_words, w4_scales, wd, wgo, offs, out):
    nc = tc.nc
    with ExitStack() as ctx:
        keep = ctx.enter_context(tc.tile_pool(name="keep", bufs=1))
        psum = ctx.enter_context(tc.psum_pool(name="psum", bufs=PSUM_BANKS))

        offsets = keep.tile([P, J // LIST_ROWS], U16, name="offsets")
        w4_codes = keep.tile([P, 2 * N], U8, name="w4_codes", align_bytes=64)
        planes = [keep.tile([P, EARLY * P], U8, name="early_plane", align_bytes=64),
                  keep.tile([P, N - EARLY * P], U8, name="late_plane", align_bytes=64)]
        wd_codes = keep.tile([P, N], U32, name="wd_codes", align_bytes=64)
        wd_plane = keep.tile([P, N], U8, name="wd_plane", align_bytes=64)
        dy_codes = keep.tile([P, J], U32, name="dy_codes", align_bytes=64)
        dy_plane = keep.tile([P, J], U8, name="dy_plane", align_bytes=64)
        weights = keep.tile([P, J], F32, name="weights")
        pages = [keep.tile([P, T], F32, name="page%d" % i) for i in range(PAGES - 1)]

        def buffer(columns, tag):
            return keep.tile([P, columns], F32, name=tag, tag=tag, align_bytes=64)

        def load(src, c0, c1, tag, sums=LEAD):
            size = PACK * (c1 - c0)
            flat = buffer(sums - LEAD + size, tag)
            raw = flat[:, sums - LEAD :].rearrange("p (t c) -> p t c", t=PACK)
            nc.sync.dma_start(out=raw, in_=src[:, c0:c1].rearrange("(p t) c -> p t c", t=PACK))
            return raw, flat[:, :sums], flat[:, size - LEAD :]

        def load_w4_scales(plane, c0, c1, quadrants=range(QUADRANTS)):
            for q in quadrants:
                nc.sync.dma_start(out=plane[32 * q : 32 * q + 4, :].bitcast(I32),
                                  in_=w4_scales[0, 4 * q : 4 * q + 4, c0:c1].bitcast(I32))

        def load_w4_words(b0, b1):
            cols = slice(b0 * P // 2, b1 * P // 2)
            nc.sync.dma_start(out=w4_codes[:].bitcast(I32)[:, cols], in_=w4_words[0].bitcast(I32)[:, cols])

        def load_weights(c0, c1):
            nc.sync.dma_start(out=weights[:, c0:c1], in_=wgo[:, c0:c1])

        def rounded(columns, tag):
            return keep.tile([P, columns, PACK], BF16, name="rounded", tag=tag, align_bytes=64)

        def weave(copy, raw, grouped, lo, hi, shift=0):
            copy(out=grouped[:, lo - shift : hi - shift, :].rearrange("p (c i) t -> p c t i", i=LINE),
                 in_=raw[:, :, lo:hi].rearrange("p t (c i) -> p c t i", i=LINE))

        def weave_lead_first(raw, tag, chunk=CHUNK):
            width = raw.shape[2]
            grouped = rounded(width, tag)
            weave(nc.scalar.copy, raw, grouped, 0, LEAD)
            for lo in range(LEAD, width, chunk):
                weave(nc.scalar.copy, raw, grouped, lo, min(lo + chunk, width))
            return grouped

        def weave_shared(raw, tag, c0, scalar_share):
            grouped = rounded(P, tag)
            weave(nc.scalar.copy, raw, grouped, c0, c0 + scalar_share, c0)
            weave(nc.vector.tensor_copy, raw, grouped, c0 + scalar_share, c0 + P, c0)
            return grouped

        def quantise(grouped, codes, plane, c0, fmt):
            lo = 0
            while lo < grouped.shape[1]:
                hi = lo + max(w for w in QUANT_WIDTHS if w <= grouped.shape[1] - lo)
                cols = slice(c0 + lo, c0 + hi)
                nc.vector.quantize_mx(out=codes[:, cols].bitcast(fmt), scales=plane[:, cols],
                                      in_=grouped[:, lo:hi, :].rearrange("p c t -> p (c t)"))
                lo = hi

        def place(b, c0, c1, sums, cuts=()):
            rows = slice(b * P, (b + 1) * P)
            w4_scale = planes[0][:, rows] if b < EARLY else planes[1][:, (b - EARLY) * P : (b - EARLY + 1) * P]
            ends = (c0, *cuts, c1)
            for lo, hi in zip(ends, ends[1:]):
                width = min(w for w in WIDTHS if w >= hi - lo)
                cols = slice(hi - width, hi)
                acc = psum.tile([P, BANK], F32, name="acc")
                moving = dy_codes[:, cols].bitcast(E5M2)
                nc.tensor.matmul_mx(out=acc[:, :width], lhsT=w4_codes[:, 2 * b * P : 2 * (b + 1) * P].bitcast(E2M1),
                                    lhsT_scale=w4_scale, rhs=moving, rhs_scale=dy_plane[:, cols],
                                    start=True, stop=False)
                nc.tensor.matmul_mx(out=acc[:, :width], lhsT=wd_codes[:, rows].bitcast(E4M3),
                                    lhsT_scale=wd_plane[:, rows], rhs=moving, rhs_scale=dy_plane[:, cols],
                                    start=False, stop=True)
                nc.scalar.copy(out=sums[:, lo - c0 : hi - c0], in_=acc[:, width - (hi - lo) : width])
            window = pages[b % PAGES][:].indirect(offsets[:, c0 // LIST_ROWS : c1 // LIST_ROWS])
            nc.vector.tensor_tensor(window, sums, weights[:, c0:c1], MULT)
            if c1 == J:
                nc.sync.dma_start(out=out[b * P : (b + 1) * P, :], in_=pages[b % PAGES][:])

        def clear_in_odd_halves(view, value):
            cut = view.shape[1] // 2 - 1
            nc.vector.memset(view[:, :cut], value)
            nc.vector.memset(view[:, cut:], value)

        clear_in_odd_halves(planes[0][:].bitcast(U32), 0)
        clear_in_odd_halves(pages[0][:], 0.0)
        clear_in_odd_halves(planes[1][:].bitcast(U32), 0)
        clear_in_odd_halves(pages[1][:, :VECTOR_CLEARS], 0.0)
        nc.gpsimd.memset(pages[1][:, VECTOR_CLEARS:], 0.0)

        width = [c1 - c0 for c0, c1 in PIECES]
        pieces = [load(dy, *PIECES[0], "dy_0")]
        load_w4_scales(planes[0], 0, EARLY * P, (0,))
        wd_01 = load(wd, 0, EARLY * P, "wd_01")[0]
        load_w4_scales(planes[0], 0, EARLY * P, (1, 2, 3))
        load_w4_words(0, EARLY)
        pieces.append(load(dy, *PIECES[1], "dy_1"))
        load_weights(0, CUTS[3])
        nc.sync.dma_start(offsets[:], offs)
        for i in range(2, len(PIECES)):
            pieces.append(load(dy, *PIECES[i], "dy_%d" % i, width[i - 1]))
        load_weights(CUTS[3], J)
        load_w4_words(EARLY, BLOCKS)

        quantise(weave_shared(pieces[0][0], "rounded_dy_0", 0, SCALAR_SHARE), dy_codes, dy_plane, 0, E5M2)
        wd_rounded = [weave_shared(wd_01, "rounded_wd_0", 0, SCALAR_SHARE), weave_shared(wd_01, "rounded_wd_1", P, P // 2)]
        for b in range(EARLY):
            quantise(wd_rounded[b], wd_codes, wd_plane, b * P, E4M3)
        grouped = rounded(width[1], "rounded_dy_1")
        weave(nc.vector.tensor_copy, pieces[1][0], grouped, 0, width[1])
        quantise(grouped, dy_codes, dy_plane, CUTS[1], E5M2)
        load_w4_scales(planes[1], EARLY * P, N)
        wd_23 = load(wd, 2 * P, 4 * P, "wd_23", width[-1])
        wd_47 = load(wd, 4 * P, N, "wd_47", J)

        for b in range(EARLY):
            place(b, *PIECES[0], buffer(width[0], "sums_%d" % b)[:])
        for i in range(1, len(PIECES) - 1):
            raw, first, second = pieces[i + 1]
            quantise(weave_lead_first(raw, "rounded_dy_%d" % (i + 1), J), dy_codes, dy_plane, CUTS[i + 1], E5M2)
            if i == len(PIECES) - 2:
                pages.append(buffer(T, "rounded_dy_%d" % (i + 1)))
                nc.gpsimd.memset(pages[-1][:], 0.0)
            place(0, *PIECES[i], first)
            place(1, *PIECES[i], second)
        quantise(weave_lead_first(wd_23[0], "rounded_wd_23"), wd_codes, wd_plane, 2 * P, E4M3)
        place(0, *PIECES[-1], wd_23[1])
        place(1, *PIECES[-1], wd_23[2])
        place(2, 0, J, buffer(J, "sums_2")[:], (BANK,))
        quantise(weave_lead_first(wd_47[0], "rounded_wd_47"), wd_codes, wd_plane, 4 * P, E4M3)
        for b in range(3, BLOCKS):
            place(b, 0, J, wd_47[1] if b == 3 else buffer(J, "sums_%d" % b)[:], (BANK,))
